import numpy as np
import ml_dtypes


def mxq(x, axis, fmt="e4m3"):
    dtype, down = {"e4m3": (ml_dtypes.float8_e4m3fn, 7), "e5m2": (ml_dtypes.float8_e5m2, 14)}[fmt]
    v = np.moveaxis(np.asarray(x, np.float32).astype(ml_dtypes.bfloat16).astype(np.float64), axis, -1)
    blocks = v.reshape(v.shape[:-1] + (-1, 32))
    amax = np.abs(blocks).max(-1, keepdims=True)
    byte = np.maximum(np.where(amax > 0, np.frexp(amax)[1] - 1 + 127, 0) - down, 1)
    scale = np.exp2(byte - 127.0)
    codes = (blocks / scale).astype(np.float32).astype(dtype).astype(np.float64)
    return np.moveaxis((codes * scale).reshape(v.shape), -1, axis)


WIDE = False


def mx_kscale(k):
    if not WIDE:
        return np.ones(k)
    levels = np.array([10, -10, 5, -5, 0])
    if k % 512:
        return np.exp2(np.random.permutation(np.resize(levels, k // 32))).repeat(32)
    a = np.empty((k // 512, 16))
    for p in range(k // 512):
        a[p, :8] = np.random.permutation(np.resize(levels, 8))
        for g in range(8):
            far = levels[np.abs(levels - a[p, g]) >= 10]
            a[p, g + 8] = far[np.random.randint(len(far))]
    return np.exp2(a.ravel()).repeat(32)


def f64(x):
    return np.asarray(x).astype(np.float64)


def striped8(idx):
    return np.concatenate([v.reshape(-1, 16).T for v in idx]).astype(np.uint16)


def unstriped8(offs):
    return np.stack([offs[16 * g:16 * g + 16].T.reshape(-1) for g in range(8)]).astype(np.int64)


def split(x):
    m, e = np.frexp(f64(x))
    hi = np.ldexp(np.trunc(16.0 * m) / 16.0, e)
    return hi, f64(x) - hi


def gelu(v):
    return 0.5 * v * (1.0 + np.tanh(np.sqrt(2.0 / np.pi) * (v + 0.044715 * v**3)))


K, M, T, S = 1024, 128, 2048, 512


def setup_inputs():
    n = np.random.standard_normal
    s = mx_kscale(K)[:, None]
    return {
        "xT": (n((K, T)) * s).astype(np.float32),
        "w": (n((K, M)) / np.sqrt(K) / s).astype(np.float32),
        "wgt": np.repeat(np.random.uniform(0.5, 2.0, (8, S)), 16, axis=0).astype(np.float32),
        "b": (0.3 * n(128)).astype(np.float32),
        "offs": striped8(np.stack([np.random.permutation(T)[:S] for _ in range(8)])),
    }


def reference(xT, w, wgt, b, offs):
    idx = unstriped8(offs)
    group = np.arange(K) % 512 // 64
    xg = f64(wgt)[np.arange(K) // 4 % 128] * f64(xT)[np.arange(K)[:, None], idx[group]]
    xT_ = mxq(xg, 0, "e4m3")
    w_hi, w_lo = split(w)
    w_hi_, w_lo_ = mxq(w_hi, 0, "e4m3"), mxq(w_lo, 0, "e4m3")
    y = w_hi_.T @ xT_ + w_lo_.T @ xT_
    return gelu(y + f64(b)[:, None])

@@ -1,0 +1,172 @@
+from contextlib import ExitStack
+
+import concourse.mybir as mybir
+from concourse.masks import make_identity
+
+F32 = mybir.dt.float32
+BF16 = mybir.dt.bfloat16
+I32 = mybir.dt.int32
+U32 = mybir.dt.uint32
+U16 = mybir.dt.uint16
+U8 = mybir.dt.uint8
+FP8X4 = mybir.dt.float8_e4m3fn_x4
+MULT = mybir.AluOpType.mult
+SUB = mybir.AluOpType.subtract
+AND = mybir.AluOpType.bitwise_and
+GELU = mybir.ActivationFunctionType.Gelu_apprx_tanh
+
+K, M, T, S = 1024, 128, 2048, 512
+P = 128
+PACK = 4
+PASSES = K // (P * PACK)
+GROUP = 16
+HALF = S // 2
+CHUNKS = ((0, 128), (128, 256), (256, 384), (384, 512))
+HEAD_BITS = -(1 << 20)
+
+FLOPS = 2 * 2 * K * M * S
+BYTES = 4 * (K * T + K * M + P // GROUP * S + M + M * S) + 2 * P * (S // GROUP)
+
+
+def tile_list_heads_hl_gelu_kernel(tc, xT, w, wgt, b, offs, out):
+    nc = tc.nc
+    with ExitStack() as ctx:
+        keep = ctx.enter_context(tc.tile_pool(name="keep", bufs=1))
+        psum = ctx.enter_context(tc.psum_pool(name="psum", bufs=1))
+
+        rows = keep.tile([P, S + M], F32, name="rows")
+        nc.vector.memset(rows[:], 0.0)
+        offsets = keep.tile([P, S // GROUP], U16, name="offsets")
+        nc.sync.dma_start(offsets[:], offs)
+        w_raw = keep.tile([P, PASSES, PACK, M], F32, name="w_raw")
+        nc.sync.dma_start(out=w_raw[:], in_=w.rearrange("(a p i) n -> p a i n", p=P, i=PACK))
+        nc.sync.dma_start(out=rows[0 : P // GROUP, 0:S], in_=wgt.rearrange("(g r) j -> g r j", r=GROUP)[:, 0, :])
+        nc.sync.dma_start(out=rows[0:1, S : S + M], in_=b.rearrange("(o n) -> o n", o=1))
+        planes_hbm = xT.rearrange("(a p i) t -> a i p t", p=P, i=PACK)
+        planes = {}
+        for a in range(PASSES):
+            for i in range(PACK):
+                planes[a, i] = keep.tile([P, T], F32, name=f"plane_{a}_{i}")
+                nc.sync.dma_start(out=planes[a, i][:], in_=planes_hbm[a, i])
+
+        identity = keep.tile([P, P], F32, name="identity")
+        make_identity(nc, identity[:])
+
+        zero = keep.tile([P, 1], F32, name="zero")
+        nc.vector.memset(zero[:], 0.0)
+        warm = keep.tile([P, 1], F32, name="warm")
+        nc.scalar.activation(warm[:], zero[:], GELU)
+
+        blocks = S // P
+        columns_ps = psum.tile([P, blocks, P], F32, name="columns_ps")
+        for c in range(blocks):
+            nc.tensor.transpose(columns_ps[:, c, :], rows[:, c * P : (c + 1) * P], identity[:])
+        bias_ps = psum.tile([P, P], F32, name="bias_ps")
+        nc.tensor.transpose(bias_ps[:], rows[:, S : S + M], identity[:])
+        repeated = keep.tile([P, blocks, P // GROUP, GROUP], F32, name="repeated")
+        nc.scalar.copy(
+            repeated[:],
+            columns_ps[:, :, 0 : P // GROUP].unsqueeze(3).to_broadcast([P, blocks, P // GROUP, GROUP]),
+        )
+        weights_ps = psum.tile([P, S], F32, name="weights_ps")
+        for c in range(blocks):
+            nc.tensor.transpose(
+                weights_ps[:, c * P : (c + 1) * P], repeated[:, c].rearrange("p g r -> p (g r)"), identity[:]
+            )
+        weights = keep.tile([P, S], F32, name="weights")
+        nc.scalar.copy(weights[:], weights_ps[:])
+        bias = keep.tile([P, 1], F32, name="bias")
+        nc.scalar.copy(bias[:], bias_ps[:, 0:1])
+
+        hi_bits = keep.tile([P, PASSES, PACK, M], I32, name="hi_bits")
+        nc.vector.tensor_scalar(hi_bits[:], w_raw[:].bitcast(I32), HEAD_BITS, None, AND)
+        hi_view = hi_bits[:].bitcast(F32).rearrange("p a i n -> p a n i")
+        w_grouped = {}
+        for name in ("hi", "lo"):
+            w_grouped[name] = keep.tile([P, PASSES, M, PACK], BF16, name=f"w_grouped_{name}", align_bytes=64)
+        nc.vector.tensor_tensor(w_grouped["lo"][:], w_raw[:].rearrange("p a i n -> p a n i"), hi_view, SUB)
+        nc.scalar.copy(w_grouped["hi"][:], hi_view)
+        w_codes, w_scales = {}, {}
+        for name in ("lo", "hi"):
+            w_codes[name] = keep.tile([P, PASSES * M], U32, name=f"w_codes_{name}", align_bytes=64)
+            w_scales[name] = keep.tile([P, PASSES * M], U8, name=f"w_scales_{name}", align_bytes=64)
+            nc.vector.quantize_mx(
+                out=w_codes[name][:].bitcast(FP8X4),
+                scales=w_scales[name][:],
+                in_=w_grouped[name][:].rearrange("p a n i -> p (a n i)"),
+            )
+
+        picked, grouped = {}, {}
+        codes = keep.tile([P, PASSES, S], U32, name="codes", align_bytes=64)
+        scales = keep.tile([P, PASSES, S], U8, name="scales", align_bytes=64)
+        for a in range(PASSES):
+            picked[a] = keep.tile([P, PACK, S], F32, name=f"picked_{a}")
+            grouped[a] = keep.tile([P, S, PACK], BF16, name=f"grouped_{a}", align_bytes=64)
+        acc = {}
+        for j0, j1 in CHUNKS:
+            acc[j0, j1] = psum.tile([M, j1 - j0], F32, name=f"acc_{j0}")
+
+        def gather(a, i, j0, j1):
+            nc.vector.tensor_tensor(
+                picked[a][:, i, j0:j1],
+                planes[a, i][:].indirect(offsets[:, j0 // GROUP : j1 // GROUP]),
+                weights[:, j0:j1],
+                MULT,
+            )
+
+        def group(copy, a, i0, i1, j0, j1):
+            copy(grouped[a][:, j0:j1, i0:i1], picked[a][:, i0:i1, j0:j1].rearrange("p i j -> p j i"))
+
+        def quantize(a, j0, j1):
+            nc.vector.quantize_mx(
+                out=codes[:, a, j0:j1].bitcast(FP8X4),
+                scales=scales[:, a, j0:j1],
+                in_=grouped[a][:, j0:j1, :].rearrange("p j i -> p (j i)"),
+            )
+
+        def multiply(a, j0, j1):
+            for name in ("lo", "hi"):
+                cols = slice(a * M, (a + 1) * M)
+                nc.tensor.matmul_mx(
+                    out=acc[j0, j1][:],
+                    lhsT=w_codes[name][:, cols].bitcast(FP8X4),
+                    lhsT_scale=w_scales[name][:, cols],
+                    rhs=codes[:, a, j0:j1].bitcast(FP8X4),
+                    rhs_scale=scales[:, a, j0:j1],
+                    start=(a == 0 and name == "lo"),
+                    stop=(a == PASSES - 1 and name == "hi"),
+                )
+
+        halves = ((0, HALF), (HALF, S))
+        for i in range(PACK):
+            for part in halves:
+                gather(0, i, *part)
+        for part in halves:
+            group(nc.scalar.copy, 0, 0, PACK, *part)
+        for part in halves:
+            gather(1, 0, *part)
+        quantize(0, 0, S)
+        for chunk in CHUNKS:
+            multiply(0, *chunk)
+        for part in halves:
+            gather(1, 1, *part)
+        for part in halves:
+            group(nc.scalar.copy, 1, 0, 2, *part)
+        for part in halves:
+            gather(1, 2, *part)
+        for j0, j1 in CHUNKS[:3]:
+            gather(1, 3, j0, j1)
+            group(nc.scalar.copy, 1, 2, PACK, j0, j1)
+        quantize(1, *CHUNKS[0])
+        multiply(1, *CHUNKS[0])
+        gather(1, 3, *CHUNKS[3])
+        quantize(1, *CHUNKS[1])
+        multiply(1, *CHUNKS[1])
+        group(nc.vector.tensor_copy, 1, 2, PACK, *CHUNKS[3])
+        for chunk in CHUNKS[2:]:
+            quantize(1, *chunk)
+            multiply(1, *chunk)
+        for j0, j1 in CHUNKS:
+            result = keep.tile([M, j1 - j0], F32, name=f"result_{j0}")
+            nc.scalar.activation(result[:], acc[j0, j1][:], GELU, bias=bias[:])
+            nc.sync.dma_start(out=out[:, j0:j1], in_=result[:])

@@ -34,20 +34,27 @@ def tile_list_heads_hl_gelu_kernel(tc, xT, w, wgt, b, offs, out):
         keep = ctx.enter_context(tc.tile_pool(name="keep", bufs=1))
         psum = ctx.enter_context(tc.psum_pool(name="psum", bufs=1))
 
-        rows = keep.tile([P, S + M], F32, name="rows")
+        rows = keep.tile([P, HALF], F32, name="rows")
         nc.vector.memset(rows[:], 0.0)
         offsets = keep.tile([P, S // GROUP], U16, name="offsets")
         nc.sync.dma_start(offsets[:], offs)
-        w_raw = keep.tile([P, PASSES, PACK, M], F32, name="w_raw")
-        nc.sync.dma_start(out=w_raw[:], in_=w.rearrange("(a p i) n -> p a i n", p=P, i=PACK))
-        nc.sync.dma_start(out=rows[0 : P // GROUP, 0:S], in_=wgt.rearrange("(g r) j -> g r j", r=GROUP)[:, 0, :])
-        nc.sync.dma_start(out=rows[0:1, S : S + M], in_=b.rearrange("(o n) -> o n", o=1))
         planes_hbm = xT.rearrange("(a p i) t -> a i p t", p=P, i=PACK)
         planes = {}
+
+        def load_plane(a, i):
+            planes[a, i] = keep.tile([P, T], F32, name=f"plane_{a}_{i}", tag=f"plane_{a}_{i}", align_bytes=64)
+            nc.sync.dma_start(out=planes[a, i][:], in_=planes_hbm[a, i])
+
+        load_plane(0, 0)
+        nc.sync.dma_start(out=rows[0:GROUP, :], in_=wgt.rearrange("p (h j) -> (p h) j", h=2)[0 : 2 * P : GROUP + 1, :])
+        w_raw = keep.tile([P, PASSES, PACK, M], F32, name="w_raw")
+        nc.sync.dma_start(out=w_raw[:], in_=w.rearrange("(a p i) n -> p a i n", p=P, i=PACK))
         for a in range(PASSES):
             for i in range(PACK):
-                planes[a, i] = keep.tile([P, T], F32, name=f"plane_{a}_{i}")
-                nc.sync.dma_start(out=planes[a, i][:], in_=planes_hbm[a, i])
+                if (a, i) not in planes:
+                    load_plane(a, i)
+        bias = keep.tile([P, 1], F32, name="bias")
+        nc.sync.dma_start(out=bias[:], in_=b.rearrange("(p o) -> p o", o=1))
 
         identity = keep.tile([P, P], F32, name="identity")
         make_identity(nc, identity[:])
@@ -57,26 +64,25 @@ def tile_list_heads_hl_gelu_kernel(tc, xT, w, wgt, b, offs, out):
         warm = keep.tile([P, 1], F32, name="warm")
         nc.scalar.activation(warm[:], zero[:], GELU)
 
-        blocks = S // P
+        blocks = HALF // P
         columns_ps = psum.tile([P, blocks, P], F32, name="columns_ps")
         for c in range(blocks):
             nc.tensor.transpose(columns_ps[:, c, :], rows[:, c * P : (c + 1) * P], identity[:])
-        bias_ps = psum.tile([P, P], F32, name="bias_ps")
-        nc.tensor.transpose(bias_ps[:], rows[:, S : S + M], identity[:])
-        repeated = keep.tile([P, blocks, P // GROUP, GROUP], F32, name="repeated")
-        nc.scalar.copy(
-            repeated[:],
-            columns_ps[:, :, 0 : P // GROUP].unsqueeze(3).to_broadcast([P, blocks, P // GROUP, GROUP]),
-        )
-        weights_ps = psum.tile([P, S], F32, name="weights_ps")
-        for c in range(blocks):
-            nc.tensor.transpose(
-                weights_ps[:, c * P : (c + 1) * P], repeated[:, c].rearrange("p g r -> p (g r)"), identity[:]
+        repeated = keep.tile([P, 2, blocks, P // GROUP, GROUP], F32, name="repeated")
+        for h in range(2):
+            nc.scalar.copy(
+                repeated[:, h],
+                columns_ps[:, :, h:GROUP:2].unsqueeze(3).to_broadcast([P, blocks, P // GROUP, GROUP]),
             )
+        weights_ps = psum.tile([P, S], F32, name="weights_ps")
+        for h in range(2):
+            for c in range(blocks):
+                j0 = h * HALF + c * P
+                nc.tensor.transpose(
+                    weights_ps[:, j0 : j0 + P], repeated[:, h, c].rearrange("p g r -> p (g r)"), identity[:]
+                )
         weights = keep.tile([P, S], F32, name="weights")
         nc.scalar.copy(weights[:], weights_ps[:])
-        bias = keep.tile([P, 1], F32, name="bias")
-        nc.scalar.copy(bias[:], bias_ps[:, 0:1])
 
         hi_bits = keep.tile([P, PASSES, PACK, M], I32, name="hi_bits")
         nc.vector.tensor_scalar(hi_bits[:], w_raw[:].bitcast(I32), HEAD_BITS, None, AND)
@@ -97,12 +103,13 @@ def tile_list_heads_hl_gelu_kernel(tc, xT, w, wgt, b, offs, out):
             )
 
         picked, grouped = {}, {}
-        codes = keep.tile([P, PASSES, S], U32, name="codes", align_bytes=64)
-        scales = keep.tile([P, PASSES, S], U8, name="scales", align_bytes=64)
+        codes, scales = {}, {}
+        codes[1] = keep.tile([P, S], U32, name="codes_1", align_bytes=64)
         for a in range(PASSES):
+            scales[a] = keep.tile([P, S], U8, name=f"scales_{a}", align_bytes=64)
             picked[a] = keep.tile([P, PACK, S], F32, name=f"picked_{a}")
             grouped[a] = keep.tile([P, S, PACK], BF16, name=f"grouped_{a}", align_bytes=64)
-        acc = {}
+        acc, results = {}, {}
         for j0, j1 in CHUNKS:
             acc[j0, j1] = psum.tile([M, j1 - j0], F32, name=f"acc_{j0}")
 
@@ -119,8 +126,8 @@ def tile_list_heads_hl_gelu_kernel(tc, xT, w, wgt, b, offs, out):
 
         def quantize(a, j0, j1):
             nc.vector.quantize_mx(
-                out=codes[:, a, j0:j1].bitcast(FP8X4),
-                scales=scales[:, a, j0:j1],
+                out=codes[a][:, j0:j1].bitcast(FP8X4),
+                scales=scales[a][:, j0:j1],
                 in_=grouped[a][:, j0:j1, :].rearrange("p j i -> p (j i)"),
             )
 
@@ -131,8 +138,8 @@ def tile_list_heads_hl_gelu_kernel(tc, xT, w, wgt, b, offs, out):
                     out=acc[j0, j1][:],
                     lhsT=w_codes[name][:, cols].bitcast(FP8X4),
                     lhsT_scale=w_scales[name][:, cols],
-                    rhs=codes[:, a, j0:j1].bitcast(FP8X4),
-                    rhs_scale=scales[:, a, j0:j1],
+                    rhs=codes[a][:, j0:j1].bitcast(FP8X4),
+                    rhs_scale=scales[a][:, j0:j1],
                     start=(a == 0 and name == "lo"),
                     stop=(a == PASSES - 1 and name == "hi"),
                 )
@@ -145,28 +152,29 @@ def tile_list_heads_hl_gelu_kernel(tc, xT, w, wgt, b, offs, out):
             group(nc.scalar.copy, 0, 0, PACK, *part)
         for part in halves:
             gather(1, 0, *part)
+        for part in halves:
+            gather(1, 1, *part)
+        group(nc.scalar.copy, 1, 0, 2, *CHUNKS[3])
+        for part in halves:
+            gather(1, 2, *part)
+        codes[0] = keep.tile([P, S], U32, name="codes_0", tag="plane_1_2", align_bytes=64)
         quantize(0, 0, S)
         for chunk in CHUNKS:
             multiply(0, *chunk)
-        for part in halves:
-            gather(1, 1, *part)
-        for part in halves:
-            group(nc.scalar.copy, 1, 0, 2, *part)
-        for part in halves:
-            gather(1, 2, *part)
+        group(nc.scalar.copy, 1, 0, 3, 0, HALF)
+        group(nc.scalar.copy, 1, 0, 3, *CHUNKS[2])
         for j0, j1 in CHUNKS[:3]:
             gather(1, 3, j0, j1)
-            group(nc.scalar.copy, 1, 2, PACK, j0, j1)
+            group(nc.scalar.copy, 1, 3, PACK, j0, j1)
+        gather(1, 3, *CHUNKS[3])
         quantize(1, *CHUNKS[0])
         multiply(1, *CHUNKS[0])
-        gather(1, 3, *CHUNKS[3])
-        quantize(1, *CHUNKS[1])
-        multiply(1, *CHUNKS[1])
         group(nc.vector.tensor_copy, 1, 2, PACK, *CHUNKS[3])
-        for chunk in CHUNKS[2:]:
-            quantize(1, *chunk)
-            multiply(1, *chunk)
-        for j0, j1 in CHUNKS:
+        for c in (1, 3, 2):
+            quantize(1, *CHUNKS[c])
+            multiply(1, *CHUNKS[c])
+        for j0, j1 in (CHUNKS[c] for c in (0, 1, 3, 2)):
             result = keep.tile([M, j1 - j0], F32, name=f"result_{j0}")
+            results[j0] = result
             nc.scalar.activation(result[:], acc[j0, j1][:], GELU, bias=bias[:])
             nc.sync.dma_start(out=out[:, j0:j1], in_=result[:])

@@ -86,27 +86,29 @@ def tile_list_heads_hl_gelu_kernel(tc, xT, w, wgt, b, offs, out):
 
         hi_bits = keep.tile([P, PASSES, PACK, M], I32, name="hi_bits")
         nc.vector.tensor_scalar(hi_bits[:], w_raw[:].bitcast(I32), HEAD_BITS, None, AND)
-        hi_view = hi_bits[:].bitcast(F32).rearrange("p a i n -> p a n i")
-        w_grouped = {}
-        for name in ("hi", "lo"):
-            w_grouped[name] = keep.tile([P, PASSES, M, PACK], BF16, name=f"w_grouped_{name}", align_bytes=64)
-        nc.vector.tensor_tensor(w_grouped["lo"][:], w_raw[:].rearrange("p a i n -> p a n i"), hi_view, SUB)
-        nc.scalar.copy(w_grouped["hi"][:], hi_view)
-        w_codes, w_scales = {}, {}
-        for name in ("lo", "hi"):
-            w_codes[name] = keep.tile([P, PASSES * M], U32, name=f"w_codes_{name}", align_bytes=64)
-            w_scales[name] = keep.tile([P, PASSES * M], U8, name=f"w_scales_{name}", align_bytes=64)
+        w_grouped, w_codes, w_scales = {}, {}, {}
+        for a in range(PASSES):
+            hi_view = hi_bits[:, a].bitcast(F32).rearrange("p i n -> p n i")
+            w_grouped[a] = keep.tile([P, 2, M, PACK], BF16, name=f"w_grouped_{a}", align_bytes=64)
+            nc.vector.tensor_tensor(w_grouped[a][:, 0], w_raw[:, a].rearrange("p i n -> p n i"), hi_view, SUB)
+            nc.scalar.copy(w_grouped[a][:, 1], hi_view)
+
+        def quantize_w(a, tag):
+            w_codes[a] = keep.tile([P, 2 * M], U32, name=f"w_codes_{a}", tag=tag, align_bytes=64)
+            w_scales[a] = keep.tile([P, 2 * M], U8, name=f"w_scales_{a}", align_bytes=64)
             nc.vector.quantize_mx(
-                out=w_codes[name][:].bitcast(FP8X4),
-                scales=w_scales[name][:],
-                in_=w_grouped[name][:].rearrange("p a n i -> p (a n i)"),
+                out=w_codes[a][:].bitcast(FP8X4),
+                scales=w_scales[a][:],
+                in_=w_grouped[a][:].rearrange("p h n i -> p (h n i)"),
             )
+
+        quantize_w(1, "w_codes_1")
 
         picked, grouped = {}, {}
         codes, scales = {}, {}
-        codes[1] = keep.tile([P, S], U32, name="codes_1", align_bytes=64)
         for a in range(PASSES):
             scales[a] = keep.tile([P, S], U8, name=f"scales_{a}", align_bytes=64)
+            codes[a] = keep.tile([P, S], U32, name=f"codes_{a}", align_bytes=64)
             picked[a] = keep.tile([P, PACK, S], F32, name=f"picked_{a}")
             grouped[a] = keep.tile([P, S, PACK], BF16, name=f"grouped_{a}", align_bytes=64)
         acc, results = {}, {}
@@ -132,16 +134,16 @@ def tile_list_heads_hl_gelu_kernel(tc, xT, w, wgt, b, offs, out):
             )
 
         def multiply(a, j0, j1):
-            for name in ("lo", "hi"):
-                cols = slice(a * M, (a + 1) * M)
+            for h in range(2):
+                cols = slice(h * M, (h + 1) * M)
                 nc.tensor.matmul_mx(
                     out=acc[j0, j1][:],
-                    lhsT=w_codes[name][:, cols].bitcast(FP8X4),
-                    lhsT_scale=w_scales[name][:, cols],
+                    lhsT=w_codes[a][:, cols].bitcast(FP8X4),
+                    lhsT_scale=w_scales[a][:, cols],
                     rhs=codes[a][:, j0:j1].bitcast(FP8X4),
                     rhs_scale=scales[a][:, j0:j1],
-                    start=(a == 0 and name == "lo"),
-                    stop=(a == PASSES - 1 and name == "hi"),
+                    start=(a == 0 and h == 0),
+                    stop=(a == PASSES - 1 and h == 1),
                 )
 
         halves = ((0, HALF), (HALF, S))
@@ -152,17 +154,18 @@ def tile_list_heads_hl_gelu_kernel(tc, xT, w, wgt, b, offs, out):
             group(nc.scalar.copy, 0, 0, PACK, *part)
         for part in halves:
             gather(1, 0, *part)
+        quantize(0, 0, S)
         for part in halves:
             gather(1, 1, *part)
-        group(nc.scalar.copy, 1, 0, 2, *CHUNKS[3])
+        for part in halves:
+            group(nc.scalar.copy, 1, 0, 2, *part)
         for part in halves:
             gather(1, 2, *part)
-        codes[0] = keep.tile([P, S], U32, name="codes_0", tag="plane_1_2", align_bytes=64)
-        quantize(0, 0, S)
+        quantize_w(0, "plane_1_2")
         for chunk in CHUNKS:
             multiply(0, *chunk)
-        group(nc.scalar.copy, 1, 0, 3, 0, HALF)
-        group(nc.scalar.copy, 1, 0, 3, *CHUNKS[2])
+        group(nc.scalar.copy, 1, 2, 3, 0, HALF)
+        group(nc.scalar.copy, 1, 2, 3, *CHUNKS[2])
         for j0, j1 in CHUNKS[:3]:
             gather(1, 3, j0, j1)
             group(nc.scalar.copy, 1, 3, PACK, j0, j1)

@@ -38,21 +38,15 @@ def tile_list_heads_hl_gelu_kernel(tc, xT, w, wgt, b, offs, out):
         nc.vector.memset(rows[:], 0.0)
         offsets = keep.tile([P, S // GROUP], U16, name="offsets")
         nc.sync.dma_start(offsets[:], offs)
-        planes_hbm = xT.rearrange("(a p i) t -> a i p t", p=P, i=PACK)
-        planes = {}
-
-        def load_plane(a, i):
-            planes[a, i] = keep.tile([P, T], F32, name=f"plane_{a}_{i}", tag=f"plane_{a}_{i}", align_bytes=64)
-            nc.sync.dma_start(out=planes[a, i][:], in_=planes_hbm[a, i])
-
-        load_plane(0, 0)
-        nc.sync.dma_start(out=rows[0:GROUP, :], in_=wgt.rearrange("p (h j) -> (p h) j", h=2)[0 : 2 * P : GROUP + 1, :])
         w_raw = keep.tile([P, PASSES, PACK, M], F32, name="w_raw")
         nc.sync.dma_start(out=w_raw[:], in_=w.rearrange("(a p i) n -> p a i n", p=P, i=PACK))
+        nc.sync.dma_start(out=rows[0:GROUP, :], in_=wgt.rearrange("p (h j) -> (p h) j", h=2)[0 : 2 * P : GROUP + 1, :])
+        planes_hbm = xT.rearrange("(a p i) t -> a i p t", p=P, i=PACK)
+        planes = {}
         for a in range(PASSES):
             for i in range(PACK):
-                if (a, i) not in planes:
-                    load_plane(a, i)
+                planes[a, i] = keep.tile([P, T], F32, name=f"plane_{a}_{i}", tag=f"plane_{a}_{i}", align_bytes=64)
+                nc.sync.dma_start(out=planes[a, i][:], in_=planes_hbm[a, i])
         bias = keep.tile([P, 1], F32, name="bias")
         nc.sync.dma_start(out=bias[:], in_=b.rearrange("(p o) -> p o", o=1))
 
@@ -68,21 +62,20 @@ def tile_list_heads_hl_gelu_kernel(tc, xT, w, wgt, b, offs, out):
         columns_ps = psum.tile([P, blocks, P], F32, name="columns_ps")
         for c in range(blocks):
             nc.tensor.transpose(columns_ps[:, c, :], rows[:, c * P : (c + 1) * P], identity[:])
+        weights = keep.tile([P, S], F32, name="weights")
         repeated = keep.tile([P, 2, blocks, P // GROUP, GROUP], F32, name="repeated")
         for h in range(2):
             nc.scalar.copy(
                 repeated[:, h],
                 columns_ps[:, :, h:GROUP:2].unsqueeze(3).to_broadcast([P, blocks, P // GROUP, GROUP]),
             )
-        weights_ps = psum.tile([P, S], F32, name="weights_ps")
         for h in range(2):
+            weights_ps = psum.tile([P, HALF], F32, name=f"weights_ps_{h}")
             for c in range(blocks):
-                j0 = h * HALF + c * P
                 nc.tensor.transpose(
-                    weights_ps[:, j0 : j0 + P], repeated[:, h, c].rearrange("p g r -> p (g r)"), identity[:]
+                    weights_ps[:, c * P : (c + 1) * P], repeated[:, h, c].rearrange("p g r -> p (g r)"), identity[:]
                 )
-        weights = keep.tile([P, S], F32, name="weights")
-        nc.scalar.copy(weights[:], weights_ps[:])
+            nc.scalar.copy(weights[:, h * HALF : (h + 1) * HALF], weights_ps[:])
 
         hi_bits = keep.tile([P, PASSES, PACK, M], I32, name="hi_bits")
         nc.vector.tensor_scalar(hi_bits[:], w_raw[:].bitcast(I32), HEAD_BITS, None, AND)
@@ -91,7 +84,7 @@ def tile_list_heads_hl_gelu_kernel(tc, xT, w, wgt, b, offs, out):
             hi_view = hi_bits[:, a].bitcast(F32).rearrange("p i n -> p n i")
             w_grouped[a] = keep.tile([P, 2, M, PACK], BF16, name=f"w_grouped_{a}", align_bytes=64)
             nc.vector.tensor_tensor(w_grouped[a][:, 0], w_raw[:, a].rearrange("p i n -> p n i"), hi_view, SUB)
-            nc.scalar.copy(w_grouped[a][:, 1], hi_view)
+            nc.vector.tensor_copy(w_grouped[a][:, 1], hi_view)
 
         def quantize_w(a, tag):
             w_codes[a] = keep.tile([P, 2 * M], U32, name=f"w_codes_{a}", tag=tag, align_bytes=64)

@@ -59,7 +59,7 @@ def tile_list_heads_hl_gelu_kernel(tc, xT, w, wgt, b, offs, out):
         nc.scalar.activation(warm[:], zero[:], GELU)
 
         blocks = HALF // P
-        columns_ps = psum.tile([P, blocks, P], F32, name="columns_ps")
+        columns_ps = psum.tile([P, blocks, P], F32, name="columns_ps", tag="columns_ps")
         for c in range(blocks):
             nc.tensor.transpose(columns_ps[:, c, :], rows[:, c * P : (c + 1) * P], identity[:])
         weights = keep.tile([P, S], F32, name="weights")
@@ -157,19 +157,32 @@ def tile_list_heads_hl_gelu_kernel(tc, xT, w, wgt, b, offs, out):
         quantize_w(0, "plane_1_2")
         for chunk in CHUNKS:
             multiply(0, *chunk)
+        for width, tag in ((P, "spare_ps"), (P // 2, "columns_ps")):
+            spare = psum.tile([M, width], F32, name=f"spare_{width}", tag=tag)
+            nc.tensor.matmul_mx(
+                out=spare[:],
+                lhsT=w_codes[0][:, 0:M].bitcast(FP8X4),
+                lhsT_scale=w_scales[0][:, 0:M],
+                rhs=codes[0][:, 0:width].bitcast(FP8X4),
+                rhs_scale=scales[0][:, 0:width],
+                start=True,
+                stop=True,
+            )
+        split = HALF + 64
         group(nc.scalar.copy, 1, 2, 3, 0, HALF)
-        group(nc.scalar.copy, 1, 2, 3, *CHUNKS[2])
+        group(nc.scalar.copy, 1, 2, 3, HALF, split)
         for j0, j1 in CHUNKS[:3]:
             gather(1, 3, j0, j1)
-            group(nc.scalar.copy, 1, 3, PACK, j0, j1)
+            group(nc.scalar.copy, 1, 3, PACK, j0, min(j1, split))
         gather(1, 3, *CHUNKS[3])
+        group(nc.vector.tensor_copy, 1, 2, PACK, split, CHUNKS[2][1])
         quantize(1, *CHUNKS[0])
         multiply(1, *CHUNKS[0])
         group(nc.vector.tensor_copy, 1, 2, PACK, *CHUNKS[3])
-        for c in (1, 3, 2):
-            quantize(1, *CHUNKS[c])
-            multiply(1, *CHUNKS[c])
-        for j0, j1 in (CHUNKS[c] for c in (0, 1, 3, 2)):
+        for chunk in CHUNKS[1:]:
+            quantize(1, *chunk)
+            multiply(1, *chunk)
+        for j0, j1 in CHUNKS:
             result = keep.tile([M, j1 - j0], F32, name=f"result_{j0}")
             results[j0] = result
             nc.scalar.activation(result[:], acc[j0, j1][:], GELU, bias=bias[:])

@@ -21,7 +21,9 @@ PACK = 4
 PASSES = K // (P * PACK)
 GROUP = 16
 HALF = S // 2
+HALVES = ((0, HALF), (HALF, S))
 CHUNKS = ((0, 128), (128, 256), (256, 384), (384, 512))
+SPLIT = HALF + 64
 HEAD_BITS = -(1 << 20)
 
 FLOPS = 2 * 2 * K * M * S
@@ -59,7 +61,7 @@ def tile_list_heads_hl_gelu_kernel(tc, xT, w, wgt, b, offs, out):
         nc.scalar.activation(warm[:], zero[:], GELU)
 
         blocks = HALF // P
-        columns_ps = psum.tile([P, blocks, P], F32, name="columns_ps", tag="columns_ps")
+        columns_ps = psum.tile([P, blocks, P], F32, name="columns_ps")
         for c in range(blocks):
             nc.tensor.transpose(columns_ps[:, c, :], rows[:, c * P : (c + 1) * P], identity[:])
         weights = keep.tile([P, S], F32, name="weights")
@@ -104,7 +106,7 @@ def tile_list_heads_hl_gelu_kernel(tc, xT, w, wgt, b, offs, out):
             codes[a] = keep.tile([P, S], U32, name=f"codes_{a}", align_bytes=64)
             picked[a] = keep.tile([P, PACK, S], F32, name=f"picked_{a}")
             grouped[a] = keep.tile([P, S, PACK], BF16, name=f"grouped_{a}", align_bytes=64)
-        acc, results = {}, {}
+        acc = {}
         for j0, j1 in CHUNKS:
             acc[j0, j1] = psum.tile([M, j1 - j0], F32, name=f"acc_{j0}")
 
@@ -116,7 +118,7 @@ def tile_list_heads_hl_gelu_kernel(tc, xT, w, wgt, b, offs, out):
                 MULT,
             )
 
-        def group(copy, a, i0, i1, j0, j1):
+        def place(copy, a, i0, i1, j0, j1):
             copy(grouped[a][:, j0:j1, i0:i1], picked[a][:, i0:i1, j0:j1].rearrange("p i j -> p j i"))
 
         def quantize(a, j0, j1):
@@ -127,63 +129,52 @@ def tile_list_heads_hl_gelu_kernel(tc, xT, w, wgt, b, offs, out):
             )
 
         def multiply(a, j0, j1):
-            for h in range(2):
-                cols = slice(h * M, (h + 1) * M)
+            for part in range(2):
+                cols = slice(part * M, (part + 1) * M)
                 nc.tensor.matmul_mx(
                     out=acc[j0, j1][:],
                     lhsT=w_codes[a][:, cols].bitcast(FP8X4),
                     lhsT_scale=w_scales[a][:, cols],
                     rhs=codes[a][:, j0:j1].bitcast(FP8X4),
                     rhs_scale=scales[a][:, j0:j1],
-                    start=(a == 0 and h == 0),
-                    stop=(a == PASSES - 1 and h == 1),
+                    start=(a == 0 and part == 0),
+                    stop=(a == PASSES - 1 and part == 1),
                 )
 
-        halves = ((0, HALF), (HALF, S))
         for i in range(PACK):
-            for part in halves:
-                gather(0, i, *part)
-        for part in halves:
-            group(nc.scalar.copy, 0, 0, PACK, *part)
-        for part in halves:
-            gather(1, 0, *part)
+            for half in HALVES:
+                gather(0, i, *half)
+        for half in HALVES:
+            place(nc.scalar.copy, 0, 0, PACK, *half)
+        for half in HALVES:
+            gather(1, 0, *half)
         quantize(0, 0, S)
-        for part in halves:
-            gather(1, 1, *part)
-        for part in halves:
-            group(nc.scalar.copy, 1, 0, 2, *part)
-        for part in halves:
-            gather(1, 2, *part)
+        for half in HALVES:
+            gather(1, 1, *half)
+        for half in HALVES:
+            place(nc.scalar.copy, 1, 0, 2, *half)
+
+        for c in (0, 3, 2, 1):
+            gather(1, 2, *CHUNKS[c])
+        place(nc.vector.tensor_copy, 1, 2, 3, SPLIT, S)
         quantize_w(0, "plane_1_2")
         for chunk in CHUNKS:
             multiply(0, *chunk)
-        for width, tag in ((P, "spare_ps"), (P // 2, "columns_ps")):
-            spare = psum.tile([M, width], F32, name=f"spare_{width}", tag=tag)
-            nc.tensor.matmul_mx(
-                out=spare[:],
-                lhsT=w_codes[0][:, 0:M].bitcast(FP8X4),
-                lhsT_scale=w_scales[0][:, 0:M],
-                rhs=codes[0][:, 0:width].bitcast(FP8X4),
-                rhs_scale=scales[0][:, 0:width],
-                start=True,
-                stop=True,
-            )
-        split = HALF + 64
-        group(nc.scalar.copy, 1, 2, 3, 0, HALF)
-        group(nc.scalar.copy, 1, 2, 3, HALF, split)
+        for j0, j1 in (CHUNKS[0], (HALF, SPLIT), CHUNKS[1]):
+            place(nc.scalar.copy, 1, 2, 3, j0, j1)
+
         for j0, j1 in CHUNKS[:3]:
             gather(1, 3, j0, j1)
-            group(nc.scalar.copy, 1, 3, PACK, j0, min(j1, split))
+            place(nc.scalar.copy, 1, 3, PACK, j0, min(j1, SPLIT))
         gather(1, 3, *CHUNKS[3])
-        group(nc.vector.tensor_copy, 1, 2, PACK, split, CHUNKS[2][1])
+        place(nc.vector.tensor_copy, 1, 3, PACK, SPLIT, CHUNKS[2][1])
         quantize(1, *CHUNKS[0])
         multiply(1, *CHUNKS[0])
-        group(nc.vector.tensor_copy, 1, 2, PACK, *CHUNKS[3])
+        place(nc.vector.tensor_copy, 1, 3, PACK, *CHUNKS[3])
         for chunk in CHUNKS[1:]:
             quantize(1, *chunk)
             multiply(1, *chunk)
         for j0, j1 in CHUNKS:
             result = keep.tile([M, j1 - j0], F32, name=f"result_{j0}")
-            results[j0] = result
             nc.scalar.activation(result[:], acc[j0, j1][:], GELU, bias=bias[:])
             nc.sync.dma_start(out=out[:, j0:j1], in_=result[:])

@@ -42,7 +42,7 @@ def tile_list_heads_hl_gelu_kernel(tc, xT, w, wgt, b, offs, out):
         nc.sync.dma_start(offsets[:], offs)
         w_raw = keep.tile([P, PASSES, PACK, M], F32, name="w_raw")
         nc.sync.dma_start(out=w_raw[:], in_=w.rearrange("(a p i) n -> p a i n", p=P, i=PACK))
-        nc.sync.dma_start(out=rows[0:GROUP, :], in_=wgt.rearrange("p (h j) -> (p h) j", h=2)[0 : 2 * P : GROUP + 1, :])
+        nc.sync.dma_start(out=rows[0:P:8, :], in_=wgt.rearrange("p (h j) -> (p h) j", h=2)[0 : 2 * P : GROUP + 1, :])
         planes_hbm = xT.rearrange("(a p i) t -> a i p t", p=P, i=PACK)
         planes = {}
         for a in range(PASSES):
@@ -69,7 +69,7 @@ def tile_list_heads_hl_gelu_kernel(tc, xT, w, wgt, b, offs, out):
         for h in range(2):
             nc.scalar.copy(
                 repeated[:, h],
-                columns_ps[:, :, h:GROUP:2].unsqueeze(3).to_broadcast([P, blocks, P // GROUP, GROUP]),
+                columns_ps[:, :, 8 * h : P : 16].unsqueeze(3).to_broadcast([P, blocks, P // GROUP, GROUP]),
             )
         for h in range(2):
             weights_ps = psum.tile([P, HALF], F32, name=f"weights_ps_{h}")
@@ -154,13 +154,13 @@ def tile_list_heads_hl_gelu_kernel(tc, xT, w, wgt, b, offs, out):
         for half in HALVES:
             place(nc.scalar.copy, 1, 0, 2, *half)
 
-        for c in (0, 3, 2, 1):
-            gather(1, 2, *CHUNKS[c])
-        place(nc.vector.tensor_copy, 1, 2, 3, SPLIT, S)
+        for cols in (CHUNKS[0], CHUNKS[1], HALVES[1]):
+            gather(1, 2, *cols)
         quantize_w(0, "plane_1_2")
+        place(nc.vector.tensor_copy, 1, 2, 3, SPLIT, S)
         for chunk in CHUNKS:
             multiply(0, *chunk)
-        for j0, j1 in (CHUNKS[0], (HALF, SPLIT), CHUNKS[1]):
+        for j0, j1 in (CHUNKS[0], CHUNKS[1], (HALF, SPLIT)):
             place(nc.scalar.copy, 1, 2, 3, j0, j1)
 
         for j0, j1 in CHUNKS[:3]:

@@ -24,6 +24,7 @@ HALF = S // 2
 HALVES = ((0, HALF), (HALF, S))
 CHUNKS = ((0, 128), (128, 256), (256, 384), (384, 512))
 SPLIT = HALF + 64
+LAST_PASS_SLOTS = (2, 0, 1, 3)
 HEAD_BITS = -(1 << 20)
 
 FLOPS = 2 * 2 * K * M * S
@@ -46,7 +47,7 @@ def tile_list_heads_hl_gelu_kernel(tc, xT, w, wgt, b, offs, out):
         planes_hbm = xT.rearrange("(a p i) t -> a i p t", p=P, i=PACK)
         planes = {}
         for a in range(PASSES):
-            for i in range(PACK):
+            for i in (range(PACK), LAST_PASS_SLOTS)[a]:
                 planes[a, i] = keep.tile([P, T], F32, name=f"plane_{a}_{i}", tag=f"plane_{a}_{i}", align_bytes=64)
                 nc.sync.dma_start(out=planes[a, i][:], in_=planes_hbm[a, i])
         bias = keep.tile([P, 1], F32, name="bias")
@@ -88,16 +89,17 @@ def tile_list_heads_hl_gelu_kernel(tc, xT, w, wgt, b, offs, out):
             nc.vector.tensor_tensor(w_grouped[a][:, 0], w_raw[:, a].rearrange("p i n -> p n i"), hi_view, SUB)
             nc.vector.tensor_copy(w_grouped[a][:, 1], hi_view)
 
-        def quantize_w(a, tag):
-            w_codes[a] = keep.tile([P, 2 * M], U32, name=f"w_codes_{a}", tag=tag, align_bytes=64)
-            w_scales[a] = keep.tile([P, 2 * M], U8, name=f"w_scales_{a}", align_bytes=64)
+        def quantize_w(a, part, tag):
+            w_codes[a, part] = keep.tile([P, M], U32, name=f"w_codes_{a}_{part}", tag=tag, align_bytes=64)
+            w_scales[a, part] = keep.tile([P, M], U8, name=f"w_scales_{a}_{part}", align_bytes=64)
             nc.vector.quantize_mx(
-                out=w_codes[a][:].bitcast(FP8X4),
-                scales=w_scales[a][:],
-                in_=w_grouped[a][:].rearrange("p h n i -> p (h n i)"),
+                out=w_codes[a, part][:].bitcast(FP8X4),
+                scales=w_scales[a, part][:],
+                in_=w_grouped[a][:, part].rearrange("p n i -> p (n i)"),
             )
 
-        quantize_w(1, "w_codes_1")
+        for a, part in ((0, 1), (1, 0), (1, 1)):
+            quantize_w(a, part, f"w_codes_{a}_{part}")
 
         picked, grouped = {}, {}
         codes, scales = {}, {}
@@ -130,11 +132,10 @@ def tile_list_heads_hl_gelu_kernel(tc, xT, w, wgt, b, offs, out):
 
         def multiply(a, j0, j1):
             for part in range(2):
-                cols = slice(part * M, (part + 1) * M)
                 nc.tensor.matmul_mx(
                     out=acc[j0, j1][:],
-                    lhsT=w_codes[a][:, cols].bitcast(FP8X4),
-                    lhsT_scale=w_scales[a][:, cols],
+                    lhsT=w_codes[a, part][:].bitcast(FP8X4),
+                    lhsT_scale=w_scales[a, part][:],
                     rhs=codes[a][:, j0:j1].bitcast(FP8X4),
                     rhs_scale=scales[a][:, j0:j1],
                     start=(a == 0 and part == 0),
@@ -147,21 +148,19 @@ def tile_list_heads_hl_gelu_kernel(tc, xT, w, wgt, b, offs, out):
         for half in HALVES:
             place(nc.scalar.copy, 0, 0, PACK, *half)
         for half in HALVES:
-            gather(1, 0, *half)
+            gather(1, 2, *half)
         quantize(0, 0, S)
-        for half in HALVES:
-            gather(1, 1, *half)
-        for half in HALVES:
-            place(nc.scalar.copy, 1, 0, 2, *half)
-
-        for cols in (CHUNKS[0], CHUNKS[1], HALVES[1]):
-            gather(1, 2, *cols)
-        quantize_w(0, "plane_1_2")
+        place(nc.scalar.copy, 1, 2, 3, 0, SPLIT)
         place(nc.vector.tensor_copy, 1, 2, 3, SPLIT, S)
+        for half in HALVES:
+            gather(1, 0, *half)
+            place(nc.scalar.copy, 1, 0, 1, *half)
+        for chunk in CHUNKS:
+            gather(1, 1, *chunk)
+            place(nc.scalar.copy, 1, 1, 2, *chunk)
+        quantize_w(0, 0, "plane_1_1")
         for chunk in CHUNKS:
             multiply(0, *chunk)
-        for j0, j1 in (CHUNKS[0], CHUNKS[1], (HALF, SPLIT)):
-            place(nc.scalar.copy, 1, 2, 3, j0, j1)
 
         for j0, j1 in CHUNKS[:3]:
             gather(1, 3, j0, j1)

@@ -23,8 +23,10 @@ GROUP = 16
 HALF = S // 2
 HALVES = ((0, HALF), (HALF, S))
 CHUNKS = ((0, 128), (128, 256), (256, 384), (384, 512))
-SPLIT = HALF + 64
+SPLIT = HALF + 96
 LAST_PASS_SLOTS = (2, 0, 1, 3)
+TAIL_ORDER = (0, 1, 3, 2)
+ROW_STEP = P // GROUP
 HEAD_BITS = -(1 << 20)
 
 FLOPS = 2 * 2 * K * M * S
@@ -40,10 +42,11 @@ def tile_list_heads_hl_gelu_kernel(tc, xT, w, wgt, b, offs, out):
         rows = keep.tile([P, HALF], F32, name="rows")
         nc.vector.memset(rows[:], 0.0)
         offsets = keep.tile([P, S // GROUP], U16, name="offsets")
-        nc.sync.dma_start(offsets[:], offs)
         w_raw = keep.tile([P, PASSES, PACK, M], F32, name="w_raw")
         nc.sync.dma_start(out=w_raw[:], in_=w.rearrange("(a p i) n -> p a i n", p=P, i=PACK))
-        nc.sync.dma_start(out=rows[0:P:8, :], in_=wgt.rearrange("p (h j) -> (p h) j", h=2)[0 : 2 * P : GROUP + 1, :])
+        nc.sync.dma_start(offsets[:], offs)
+        half_rows = wgt.rearrange("p (h j) -> (p h) j", h=2)
+        nc.sync.dma_start(out=rows[0:P:ROW_STEP, :], in_=half_rows[0 : 2 * P : GROUP + 1, :])
         planes_hbm = xT.rearrange("(a p i) t -> a i p t", p=P, i=PACK)
         planes = {}
         for a in range(PASSES):
@@ -70,7 +73,9 @@ def tile_list_heads_hl_gelu_kernel(tc, xT, w, wgt, b, offs, out):
         for h in range(2):
             nc.scalar.copy(
                 repeated[:, h],
-                columns_ps[:, :, 8 * h : P : 16].unsqueeze(3).to_broadcast([P, blocks, P // GROUP, GROUP]),
+                columns_ps[:, :, ROW_STEP * h : P : 2 * ROW_STEP]
+                .unsqueeze(3)
+                .to_broadcast([P, blocks, P // GROUP, GROUP]),
             )
         for h in range(2):
             weights_ps = psum.tile([P, HALF], F32, name=f"weights_ps_{h}")
@@ -162,18 +167,19 @@ def tile_list_heads_hl_gelu_kernel(tc, xT, w, wgt, b, offs, out):
         for chunk in CHUNKS:
             multiply(0, *chunk)
 
+        for c in TAIL_ORDER:
+            gather(1, 3, *CHUNKS[c])
         for j0, j1 in CHUNKS[:3]:
-            gather(1, 3, j0, j1)
             place(nc.scalar.copy, 1, 3, PACK, j0, min(j1, SPLIT))
-        gather(1, 3, *CHUNKS[3])
-        place(nc.vector.tensor_copy, 1, 3, PACK, SPLIT, CHUNKS[2][1])
         quantize(1, *CHUNKS[0])
         multiply(1, *CHUNKS[0])
         place(nc.vector.tensor_copy, 1, 3, PACK, *CHUNKS[3])
-        for chunk in CHUNKS[1:]:
-            quantize(1, *chunk)
-            multiply(1, *chunk)
-        for j0, j1 in CHUNKS:
+        place(nc.vector.tensor_copy, 1, 3, PACK, SPLIT, CHUNKS[2][1])
+        for c in TAIL_ORDER[1:]:
+            quantize(1, *CHUNKS[c])
+            multiply(1, *CHUNKS[c])
+        for c in TAIL_ORDER:
+            j0, j1 = CHUNKS[c]
             result = keep.tile([M, j1 - j0], F32, name=f"result_{j0}")
             nc.scalar.activation(result[:], acc[j0, j1][:], GELU, bias=bias[:])
             nc.sync.dma_start(out=out[:, j0:j1], in_=result[:])

@@ -24,7 +24,7 @@ HALF = S // 2
 HALVES = ((0, HALF), (HALF, S))
 CHUNKS = ((0, 128), (128, 256), (256, 384), (384, 512))
 SPLIT = HALF + 96
-LAST_PASS_SLOTS = (2, 0, 1, 3)
+MOVE_SPLIT = 1152
 TAIL_ORDER = (0, 1, 3, 2)
 ROW_STEP = P // GROUP
 HEAD_BITS = -(1 << 20)
@@ -47,12 +47,15 @@ def tile_list_heads_hl_gelu_kernel(tc, xT, w, wgt, b, offs, out):
         nc.sync.dma_start(offsets[:], offs)
         half_rows = wgt.rearrange("p (h j) -> (p h) j", h=2)
         nc.sync.dma_start(out=rows[0:P:ROW_STEP, :], in_=half_rows[0 : 2 * P : GROUP + 1, :])
+        pairs_hbm = xT.rearrange("(a p u e) t -> a u p (e t)", p=P, u=2, e=2)
         planes_hbm = xT.rearrange("(a p i) t -> a i p t", p=P, i=PACK)
-        planes = {}
-        for a in range(PASSES):
-            for i in (range(PACK), LAST_PASS_SLOTS)[a]:
-                planes[a, i] = keep.tile([P, T], F32, name=f"plane_{a}_{i}", tag=f"plane_{a}_{i}", align_bytes=64)
-                nc.sync.dma_start(out=planes[a, i][:], in_=planes_hbm[a, i])
+        pairs, planes = {}, {}
+        for u in range(2):
+            pairs[u] = keep.tile([P, 2 * T], F32, name=f"pair_{u}", tag=f"pair_{u}", align_bytes=64)
+            nc.sync.dma_start(out=pairs[u][:], in_=pairs_hbm[0, u])
+        for i in range(PACK):
+            planes[i] = keep.tile([P, T], F32, name=f"plane_{i}", tag=f"plane_{i}", align_bytes=64)
+            nc.sync.dma_start(out=planes[i][:], in_=planes_hbm[1, i])
         bias = keep.tile([P, 1], F32, name="bias")
         nc.sync.dma_start(out=bias[:], in_=b.rearrange("(p o) -> p o", o=1))
 
@@ -69,7 +72,7 @@ def tile_list_heads_hl_gelu_kernel(tc, xT, w, wgt, b, offs, out):
         for c in range(blocks):
             nc.tensor.transpose(columns_ps[:, c, :], rows[:, c * P : (c + 1) * P], identity[:])
         weights = keep.tile([P, S], F32, name="weights")
-        repeated = keep.tile([P, 2, blocks, P // GROUP, GROUP], F32, name="repeated")
+        repeated = keep.tile([P, 2, blocks, P // GROUP, GROUP], F32, name="repeated", tag="moved")
         for h in range(2):
             nc.scalar.copy(
                 repeated[:, h],
@@ -84,6 +87,8 @@ def tile_list_heads_hl_gelu_kernel(tc, xT, w, wgt, b, offs, out):
                     weights_ps[:, c * P : (c + 1) * P], repeated[:, h, c].rearrange("p g r -> p (g r)"), identity[:]
                 )
             nc.scalar.copy(weights[:, h * HALF : (h + 1) * HALF], weights_ps[:])
+
+        shared = keep.tile([P, 3 * S], F32, name="shared", align_bytes=64)
 
         hi_bits = keep.tile([P, PASSES, PACK, M], I32, name="hi_bits")
         nc.vector.tensor_scalar(hi_bits[:], w_raw[:].bitcast(I32), HEAD_BITS, None, AND)
@@ -106,33 +111,30 @@ def tile_list_heads_hl_gelu_kernel(tc, xT, w, wgt, b, offs, out):
         for a, part in ((0, 1), (1, 0), (1, 1)):
             quantize_w(a, part, f"w_codes_{a}_{part}")
 
-        picked, grouped = {}, {}
         codes, scales = {}, {}
         for a in range(PASSES):
             scales[a] = keep.tile([P, S], U8, name=f"scales_{a}", align_bytes=64)
             codes[a] = keep.tile([P, S], U32, name=f"codes_{a}", align_bytes=64)
-            picked[a] = keep.tile([P, PACK, S], F32, name=f"picked_{a}")
-            grouped[a] = keep.tile([P, S, PACK], BF16, name=f"grouped_{a}", align_bytes=64)
+        grouped_last = keep.tile([P, S * PACK], BF16, name="grouped_last", align_bytes=64)
+        grouped = (shared[:, 0 : 2 * S].bitcast(BF16), grouped_last[:])
         acc = {}
         for j0, j1 in CHUNKS:
             acc[j0, j1] = psum.tile([M, j1 - j0], F32, name=f"acc_{j0}")
 
-        def gather(a, i, j0, j1):
+        def gather(products, window, j0, j1):
             nc.vector.tensor_tensor(
-                picked[a][:, i, j0:j1],
-                planes[a, i][:].indirect(offsets[:, j0 // GROUP : j1 // GROUP]),
-                weights[:, j0:j1],
-                MULT,
+                products[:, j0:j1], window[:].indirect(offsets[:, j0 // GROUP : j1 // GROUP]), weights[:, j0:j1], MULT
             )
 
-        def place(copy, a, i0, i1, j0, j1):
-            copy(grouped[a][:, j0:j1, i0:i1], picked[a][:, i0:i1, j0:j1].rearrange("p i j -> p j i"))
+        def place(copy, a, i0, products, j0, j1):
+            slots = grouped[a].rearrange("p (j i) -> p j i", i=PACK)
+            copy(slots[:, j0:j1, i0 : i0 + products.shape[1]], products[:, :, j0:j1].rearrange("p i j -> p j i"))
 
         def quantize(a, j0, j1):
             nc.vector.quantize_mx(
                 out=codes[a][:, j0:j1].bitcast(FP8X4),
                 scales=scales[a][:, j0:j1],
-                in_=grouped[a][:, j0:j1, :].rearrange("p j i -> p (j i)"),
+                in_=grouped[a][:, j0 * PACK : j1 * PACK],
             )
 
         def multiply(a, j0, j1):
@@ -147,34 +149,42 @@ def tile_list_heads_hl_gelu_kernel(tc, xT, w, wgt, b, offs, out):
                     stop=(a == PASSES - 1 and part == 1),
                 )
 
-        for i in range(PACK):
+        for u in range(2):
+            moved = keep.tile([P, T], F32, name=f"moved_{u}", tag="moved")
+            nc.scalar.copy(moved[:, 0:MOVE_SPLIT], pairs[u][:, T : T + MOVE_SPLIT])
+            nc.vector.tensor_copy(moved[:, MOVE_SPLIT:T], pairs[u][:, T + MOVE_SPLIT : 2 * T])
+            products = keep.tile([P, 2, S], F32, name=f"products_{u}", tag=("products_0", "pair_0")[u], align_bytes=64)
             for half in HALVES:
-                gather(0, i, *half)
+                gather(products[:, 0], pairs[u], *half)
+            for half in HALVES:
+                gather(products[:, 1], moved, *half)
+                place(nc.scalar.copy, 0, 2 * u, products, *half)
+
+        products = keep.tile([P, 2, S], F32, name="products_2", tag="pair_1", align_bytes=64)
         for half in HALVES:
-            place(nc.scalar.copy, 0, 0, PACK, *half)
-        for half in HALVES:
-            gather(1, 2, *half)
+            gather(products[:, 0], planes[0], *half)
         quantize(0, 0, S)
-        place(nc.scalar.copy, 1, 2, 3, 0, SPLIT)
-        place(nc.vector.tensor_copy, 1, 2, 3, SPLIT, S)
         for half in HALVES:
-            gather(1, 0, *half)
-            place(nc.scalar.copy, 1, 0, 1, *half)
-        for chunk in CHUNKS:
-            gather(1, 1, *chunk)
-            place(nc.scalar.copy, 1, 1, 2, *chunk)
-        quantize_w(0, 0, "plane_1_1")
+            gather(products[:, 1], planes[1], *half)
+            place(nc.scalar.copy, 1, 0, products, *half)
+        products = shared[:, S : 3 * S].rearrange("p (i j) -> p i j", i=2)
+        gather(products[:, 0], planes[2], SPLIT, S)
+        for j0, j1 in ((0, SPLIT - (S - SPLIT)), (SPLIT - (S - SPLIT), SPLIT)):
+            gather(products[:, 0], planes[2], j0, j1)
+            place(nc.scalar.copy, 1, 2, products[:, 0:1], j0, j1)
+        place(nc.vector.tensor_copy, 1, 2, products[:, 0:1], SPLIT, S)
+        quantize_w(0, 0, "plane_2")
         for chunk in CHUNKS:
             multiply(0, *chunk)
 
         for c in TAIL_ORDER:
-            gather(1, 3, *CHUNKS[c])
+            gather(products[:, 1], planes[3], *CHUNKS[c])
         for j0, j1 in CHUNKS[:3]:
-            place(nc.scalar.copy, 1, 3, PACK, j0, min(j1, SPLIT))
+            place(nc.scalar.copy, 1, 3, products[:, 1:2], j0, min(j1, SPLIT))
         quantize(1, *CHUNKS[0])
         multiply(1, *CHUNKS[0])
-        place(nc.vector.tensor_copy, 1, 3, PACK, *CHUNKS[3])
-        place(nc.vector.tensor_copy, 1, 3, PACK, SPLIT, CHUNKS[2][1])
+        place(nc.vector.tensor_copy, 1, 3, products[:, 1:2], *CHUNKS[3])
+        place(nc.vector.tensor_copy, 1, 3, products[:, 1:2], SPLIT, CHUNKS[2][1])
         for c in TAIL_ORDER[1:]:
             quantize(1, *CHUNKS[c])
             multiply(1, *CHUNKS[c])

@@ -24,7 +24,7 @@ HALF = S // 2
 HALVES = ((0, HALF), (HALF, S))
 CHUNKS = ((0, 128), (128, 256), (256, 384), (384, 512))
 SPLIT = HALF + 96
-MOVE_SPLIT = 1152
+MOVE_SPLIT = 1280
 TAIL_ORDER = (0, 1, 3, 2)
 ROW_STEP = P // GROUP
 HEAD_BITS = -(1 << 20)
@@ -57,7 +57,8 @@ def tile_list_heads_hl_gelu_kernel(tc, xT, w, wgt, b, offs, out):
             planes[i] = keep.tile([P, T], F32, name=f"plane_{i}", tag=f"plane_{i}", align_bytes=64)
             nc.sync.dma_start(out=planes[i][:], in_=planes_hbm[1, i])
         bias = keep.tile([P, 1], F32, name="bias")
-        nc.sync.dma_start(out=bias[:], in_=b.rearrange("(p o) -> p o", o=1))
+        for p0 in (0, P // 2):
+            nc.sync.dma_start(out=bias[p0 : p0 + P // 2], in_=b.rearrange("(p o) -> p o", o=1)[p0 : p0 + P // 2])
 
         identity = keep.tile([P, P], F32, name="identity")
         make_identity(nc, identity[:])
@@ -163,10 +164,10 @@ def tile_list_heads_hl_gelu_kernel(tc, xT, w, wgt, b, offs, out):
         products = keep.tile([P, 2, S], F32, name="products_2", tag="pair_1", align_bytes=64)
         for half in HALVES:
             gather(products[:, 0], planes[0], *half)
-        quantize(0, 0, S)
         for half in HALVES:
             gather(products[:, 1], planes[1], *half)
             place(nc.scalar.copy, 1, 0, products, *half)
+        quantize(0, 0, S)
         products = shared[:, S : 3 * S].rearrange("p (i j) -> p i j", i=2)
         gather(products[:, 0], planes[2], SPLIT, S)
         for j0, j1 in ((0, SPLIT - (S - SPLIT)), (SPLIT - (S - SPLIT), SPLIT)):

@@ -22,10 +22,12 @@ PASSES = K // (P * PACK)
 GROUP = 16
 HALF = S // 2
 HALVES = ((0, HALF), (HALF, S))
-CHUNKS = ((0, 128), (128, 256), (256, 384), (384, 512))
-SPLIT = HALF + 96
+CHUNK = 128
+CHUNKS = tuple((j0, j0 + CHUNK) for j0 in range(0, S, CHUNK))
+SPLIT = S - 32
+FINISH_ORDER = (0, 2, 1, 3)
 MOVE_SPLIT = 1280
-TAIL_ORDER = (0, 1, 3, 2)
+PLANE = 4 * T
 ROW_STEP = P // GROUP
 HEAD_BITS = -(1 << 20)
 
@@ -37,32 +39,31 @@ def tile_list_heads_hl_gelu_kernel(tc, xT, w, wgt, b, offs, out):
     nc = tc.nc
     with ExitStack() as ctx:
         keep = ctx.enter_context(tc.tile_pool(name="keep", bufs=1))
+        placed = ctx.enter_context(tc.tile_pool(name="placed", bufs=1))
         psum = ctx.enter_context(tc.psum_pool(name="psum", bufs=1))
 
-        rows = keep.tile([P, HALF], F32, name="rows")
+        def at(planes_in, shape, dtype, name):
+            return placed.tile(shape, dtype, name=name, align_bytes=PLANE, offset=planes_in * PLANE)
+
+        rows = keep.tile([P, HALF], F32, name="rows", align_bytes=4 * HALF)
         nc.vector.memset(rows[:], 0.0)
-        offsets = keep.tile([P, S // GROUP], U16, name="offsets")
-        w_raw = keep.tile([P, PASSES, PACK, M], F32, name="w_raw")
+        w_raw = keep.tile([P, PASSES, PACK, M], F32, name="w_raw", align_bytes=4 * PASSES * PACK * M)
         nc.sync.dma_start(out=w_raw[:], in_=w.rearrange("(a p i) n -> p a i n", p=P, i=PACK))
+        offsets = keep.tile([P, S // GROUP], U16, name="offsets", align_bytes=2 * S // GROUP)
         nc.sync.dma_start(offsets[:], offs)
         half_rows = wgt.rearrange("p (h j) -> (p h) j", h=2)
         nc.sync.dma_start(out=rows[0:P:ROW_STEP, :], in_=half_rows[0 : 2 * P : GROUP + 1, :])
         pairs_hbm = xT.rearrange("(a p u e) t -> a u p (e t)", p=P, u=2, e=2)
         planes_hbm = xT.rearrange("(a p i) t -> a i p t", p=P, i=PACK)
-        pairs, planes = {}, {}
+        pairs = [at(4 * u, [P, 2 * T], F32, f"pair_{u}") for u in range(2)]
+        planes = [at(place_of, [P, T], F32, f"plane_{i}") for i, place_of in enumerate((2, 3, 6, 7))]
         for u in range(2):
-            pairs[u] = keep.tile([P, 2 * T], F32, name=f"pair_{u}", tag=f"pair_{u}", align_bytes=64)
             nc.sync.dma_start(out=pairs[u][:], in_=pairs_hbm[0, u])
         for i in range(PACK):
-            planes[i] = keep.tile([P, T], F32, name=f"plane_{i}", tag=f"plane_{i}", align_bytes=64)
             nc.sync.dma_start(out=planes[i][:], in_=planes_hbm[1, i])
-        bias = keep.tile([P, 1], F32, name="bias")
-        for p0 in (0, P // 2):
-            nc.sync.dma_start(out=bias[p0 : p0 + P // 2], in_=b.rearrange("(p o) -> p o", o=1)[p0 : p0 + P // 2])
 
         identity = keep.tile([P, P], F32, name="identity")
         make_identity(nc, identity[:])
-
         zero = keep.tile([P, 1], F32, name="zero")
         nc.vector.memset(zero[:], 0.0)
         warm = keep.tile([P, 1], F32, name="warm")
@@ -73,7 +74,7 @@ def tile_list_heads_hl_gelu_kernel(tc, xT, w, wgt, b, offs, out):
         for c in range(blocks):
             nc.tensor.transpose(columns_ps[:, c, :], rows[:, c * P : (c + 1) * P], identity[:])
         weights = keep.tile([P, S], F32, name="weights")
-        repeated = keep.tile([P, 2, blocks, P // GROUP, GROUP], F32, name="repeated", tag="moved")
+        repeated = at(8, [P, 2, blocks, P // GROUP, GROUP], F32, "repeated")
         for h in range(2):
             nc.scalar.copy(
                 repeated[:, h],
@@ -89,47 +90,43 @@ def tile_list_heads_hl_gelu_kernel(tc, xT, w, wgt, b, offs, out):
                 )
             nc.scalar.copy(weights[:, h * HALF : (h + 1) * HALF], weights_ps[:])
 
-        shared = keep.tile([P, 3 * S], F32, name="shared", align_bytes=64)
-
         hi_bits = keep.tile([P, PASSES, PACK, M], I32, name="hi_bits")
         nc.vector.tensor_scalar(hi_bits[:], w_raw[:].bitcast(I32), HEAD_BITS, None, AND)
-        w_grouped, w_codes, w_scales = {}, {}, {}
+        w_grouped = keep.tile([P, PASSES, 2, M, PACK], BF16, name="w_grouped", align_bytes=64)
         for a in range(PASSES):
             hi_view = hi_bits[:, a].bitcast(F32).rearrange("p i n -> p n i")
-            w_grouped[a] = keep.tile([P, 2, M, PACK], BF16, name=f"w_grouped_{a}", align_bytes=64)
-            nc.vector.tensor_tensor(w_grouped[a][:, 0], w_raw[:, a].rearrange("p i n -> p n i"), hi_view, SUB)
-            nc.vector.tensor_copy(w_grouped[a][:, 1], hi_view)
+            nc.vector.tensor_tensor(w_grouped[:, a, 0], w_raw[:, a].rearrange("p i n -> p n i"), hi_view, SUB)
+            nc.vector.tensor_copy(w_grouped[:, a, 1], hi_view)
+        w_codes, w_scales = {}, {}
 
-        def quantize_w(a, part, tag):
-            w_codes[a, part] = keep.tile([P, M], U32, name=f"w_codes_{a}_{part}", tag=tag, align_bytes=64)
+        def quantize_w(a, part, words):
+            w_codes[a, part] = words
             w_scales[a, part] = keep.tile([P, M], U8, name=f"w_scales_{a}_{part}", align_bytes=64)
             nc.vector.quantize_mx(
-                out=w_codes[a, part][:].bitcast(FP8X4),
+                out=words[:].bitcast(FP8X4),
                 scales=w_scales[a, part][:],
-                in_=w_grouped[a][:, part].rearrange("p n i -> p (n i)"),
+                in_=w_grouped[:, a, part].rearrange("p n i -> p (n i)"),
             )
 
         for a, part in ((0, 1), (1, 0), (1, 1)):
-            quantize_w(a, part, f"w_codes_{a}_{part}")
+            quantize_w(a, part, keep.tile([P, M], U32, name=f"w_codes_{a}_{part}", align_bytes=64))
 
-        codes, scales = {}, {}
-        for a in range(PASSES):
-            scales[a] = keep.tile([P, S], U8, name=f"scales_{a}", align_bytes=64)
-            codes[a] = keep.tile([P, S], U32, name=f"codes_{a}", align_bytes=64)
-        grouped_last = keep.tile([P, S * PACK], BF16, name="grouped_last", align_bytes=64)
-        grouped = (shared[:, 0 : 2 * S].bitcast(BF16), grouped_last[:])
-        acc = {}
-        for j0, j1 in CHUNKS:
-            acc[j0, j1] = psum.tile([M, j1 - j0], F32, name=f"acc_{j0}")
+        codes = [keep.tile([P, S], U32, name=f"codes_{a}", align_bytes=64) for a in range(PASSES)]
+        scales = [keep.tile([P, S], U8, name=f"scales_{a}", align_bytes=64) for a in range(PASSES)]
+        grouped_first = keep.tile([P, S * PACK], BF16, name="grouped_first", align_bytes=64)
+        tail_words = keep.tile([P, 2 * SPLIT + CHUNK], F32, name="tail_words", align_bytes=64)
+        grouped = [grouped_first[:], tail_words[:, 0 : 2 * S].bitcast(BF16)]
+        first_products = tail_words[:, 2 * SPLIT : 2 * SPLIT + CHUNK]
+        acc = [psum.tile([M, CHUNK], F32, name=f"acc_{c}") for c in range(len(CHUNKS))]
 
         def gather(products, window, j0, j1):
             nc.vector.tensor_tensor(
-                products[:, j0:j1], window[:].indirect(offsets[:, j0 // GROUP : j1 // GROUP]), weights[:, j0:j1], MULT
+                products, window[:].indirect(offsets[:, j0 // GROUP : j1 // GROUP]), weights[:, j0:j1], MULT
             )
 
         def place(copy, a, i0, products, j0, j1):
             slots = grouped[a].rearrange("p (j i) -> p j i", i=PACK)
-            copy(slots[:, j0:j1, i0 : i0 + products.shape[1]], products[:, :, j0:j1].rearrange("p i j -> p j i"))
+            copy(slots[:, j0:j1, i0 : i0 + products.shape[1]], products.rearrange("p i j -> p j i"))
 
         def quantize(a, j0, j1):
             nc.vector.quantize_mx(
@@ -138,10 +135,11 @@ def tile_list_heads_hl_gelu_kernel(tc, xT, w, wgt, b, offs, out):
                 in_=grouped[a][:, j0 * PACK : j1 * PACK],
             )
 
-        def multiply(a, j0, j1):
+        def multiply(a, c):
+            j0, j1 = CHUNKS[c]
             for part in range(2):
                 nc.tensor.matmul_mx(
-                    out=acc[j0, j1][:],
+                    out=acc[c][:],
                     lhsT=w_codes[a, part][:].bitcast(FP8X4),
                     lhsT_scale=w_scales[a, part][:],
                     rhs=codes[a][:, j0:j1].bitcast(FP8X4),
@@ -151,46 +149,53 @@ def tile_list_heads_hl_gelu_kernel(tc, xT, w, wgt, b, offs, out):
                 )
 
         for u in range(2):
-            moved = keep.tile([P, T], F32, name=f"moved_{u}", tag="moved")
+            moved = at(8, [P, T], F32, f"moved_{u}")
             nc.scalar.copy(moved[:, 0:MOVE_SPLIT], pairs[u][:, T : T + MOVE_SPLIT])
             nc.vector.tensor_copy(moved[:, MOVE_SPLIT:T], pairs[u][:, T + MOVE_SPLIT : 2 * T])
-            products = keep.tile([P, 2, S], F32, name=f"products_{u}", tag=("products_0", "pair_0")[u], align_bytes=64)
-            for half in HALVES:
-                gather(products[:, 0], pairs[u], *half)
-            for half in HALVES:
-                gather(products[:, 1], moved, *half)
-                place(nc.scalar.copy, 0, 2 * u, products, *half)
+            products = at((9, 0)[u], [P, 2, S], F32, f"products_{u}")
+            for j0, j1 in HALVES:
+                gather(products[:, 0, j0:j1], pairs[u], j0, j1)
+            for j0, j1 in HALVES:
+                gather(products[:, 1, j0:j1], moved, j0, j1)
+                place(nc.scalar.copy, 0, 2 * u, products[:, :, j0:j1], j0, j1)
 
-        products = keep.tile([P, 2, S], F32, name="products_2", tag="pair_1", align_bytes=64)
-        for half in HALVES:
-            gather(products[:, 0], planes[0], *half)
-        for half in HALVES:
-            gather(products[:, 1], planes[1], *half)
-            place(nc.scalar.copy, 1, 0, products, *half)
+        products = at(5, [P, PACK, S], F32, "products_2")
+        for j0, j1 in HALVES:
+            gather(products[:, 0, j0:j1], planes[0], j0, j1)
         quantize(0, 0, S)
-        products = shared[:, S : 3 * S].rearrange("p (i j) -> p i j", i=2)
-        gather(products[:, 0], planes[2], SPLIT, S)
-        for j0, j1 in ((0, SPLIT - (S - SPLIT)), (SPLIT - (S - SPLIT), SPLIT)):
-            gather(products[:, 0], planes[2], j0, j1)
-            place(nc.scalar.copy, 1, 2, products[:, 0:1], j0, j1)
-        place(nc.vector.tensor_copy, 1, 2, products[:, 0:1], SPLIT, S)
-        quantize_w(0, 0, "plane_2")
-        for chunk in CHUNKS:
-            multiply(0, *chunk)
+        for j0, j1 in HALVES:
+            gather(products[:, 1, j0:j1], planes[1], j0, j1)
+            place(nc.scalar.copy, 1, 0, products[:, 0:2, j0 : min(j1, SPLIT)], j0, min(j1, SPLIT))
 
-        for c in TAIL_ORDER:
-            gather(products[:, 1], planes[3], *CHUNKS[c])
-        for j0, j1 in CHUNKS[:3]:
-            place(nc.scalar.copy, 1, 3, products[:, 1:2], j0, min(j1, SPLIT))
-        quantize(1, *CHUNKS[0])
-        multiply(1, *CHUNKS[0])
-        place(nc.vector.tensor_copy, 1, 3, products[:, 1:2], *CHUNKS[3])
-        place(nc.vector.tensor_copy, 1, 3, products[:, 1:2], SPLIT, CHUNKS[2][1])
-        for c in TAIL_ORDER[1:]:
-            quantize(1, *CHUNKS[c])
-            multiply(1, *CHUNKS[c])
-        for c in TAIL_ORDER:
+        reused = at(1, [P, 3 * T + 8], F32, "reused")
+        bias = reused[:, 0:1]
+        for p0 in (0, P // 2):
+            nc.sync.dma_start(out=bias[p0 : p0 + P // 2], in_=b.rearrange("(p o) -> p o", o=1)[p0 : p0 + P // 2])
+
+        for c in (2, 0, 1, 3):
             j0, j1 = CHUNKS[c]
-            result = keep.tile([M, j1 - j0], F32, name=f"result_{j0}")
-            nc.scalar.activation(result[:], acc[j0, j1][:], GELU, bias=bias[:])
+            gather(products[:, 2, j0:j1], planes[2], j0, j1)
+            if c != 2:
+                place(nc.scalar.copy, 1, 2, products[:, 2:3, j0 : min(j1, SPLIT)], j0, min(j1, SPLIT))
+        place(nc.vector.tensor_copy, 1, 2, products[:, 2:3, CHUNKS[2][0] : CHUNKS[2][1]], *CHUNKS[2])
+        quantize_w(0, 0, at(6, [P, M], U32, "w_codes_0_0"))
+        for c in range(len(CHUNKS)):
+            multiply(0, c)
+
+        for c, (j0, j1) in enumerate(CHUNKS):
+            gather(products[:, 3, j0:j1] if c else first_products, planes[3], j0, j1)
+        place(nc.scalar.copy, 1, 3, first_products.unsqueeze(1), *CHUNKS[0])
+        for j0, j1 in (CHUNKS[1], (CHUNKS[3][0], SPLIT)):
+            place(nc.scalar.copy, 1, 3, products[:, 3:4, j0:j1], j0, j1)
+        place(nc.vector.tensor_copy, 1, 3, products[:, 3:4, CHUNKS[2][0] : CHUNKS[2][1]], *CHUNKS[2])
+        quantize(1, *CHUNKS[0])
+        multiply(1, 0)
+        place(nc.vector.tensor_copy, 1, 0, products[:, :, SPLIT:S], SPLIT, S)
+        for c in FINISH_ORDER[1:]:
+            quantize(1, *CHUNKS[c])
+            multiply(1, c)
+        for c in FINISH_ORDER:
+            j0, j1 = CHUNKS[c]
+            result = keep.tile([M, CHUNK], F32, name=f"result_{c}", align_bytes=4 * CHUNK)
+            nc.scalar.activation(result[:], acc[c][:], GELU, bias=bias)
             nc.sync.dma_start(out=out[:, j0:j1], in_=result[:])

@@ -24,9 +24,9 @@ HALF = S // 2
 HALVES = ((0, HALF), (HALF, S))
 CHUNK = 128
 CHUNKS = tuple((j0, j0 + CHUNK) for j0 in range(0, S, CHUNK))
-SPLIT = S - 32
-FINISH_ORDER = (0, 2, 1, 3)
-MOVE_SPLIT = 1280
+OWN = (3 * CHUNK - 80, 3 * CHUNK)
+SPLIT = S - 56
+MOVE_SPLIT = 1440
 PLANE = 4 * T
 ROW_STEP = P // GROUP
 HEAD_BITS = -(1 << 20)
@@ -53,14 +53,14 @@ def tile_list_heads_hl_gelu_kernel(tc, xT, w, wgt, b, offs, out):
         nc.sync.dma_start(offsets[:], offs)
         half_rows = wgt.rearrange("p (h j) -> (p h) j", h=2)
         nc.sync.dma_start(out=rows[0:P:ROW_STEP, :], in_=half_rows[0 : 2 * P : GROUP + 1, :])
-        pairs_hbm = xT.rearrange("(a p u e) t -> a u p (e t)", p=P, u=2, e=2)
         planes_hbm = xT.rearrange("(a p i) t -> a i p t", p=P, i=PACK)
-        pairs = [at(4 * u, [P, 2 * T], F32, f"pair_{u}") for u in range(2)]
-        planes = [at(place_of, [P, T], F32, f"plane_{i}") for i, place_of in enumerate((2, 3, 6, 7))]
-        for u in range(2):
-            nc.sync.dma_start(out=pairs[u][:], in_=pairs_hbm[0, u])
-        for i in range(PACK):
-            nc.sync.dma_start(out=planes[i][:], in_=planes_hbm[1, i])
+        pair = at(0, [P, 2 * T], F32, "pair")
+        nc.sync.dma_start(out=pair[:], in_=xT.rearrange("(a p u e) t -> a u p (e t)", p=P, u=2, e=2)[0, 0])
+        planes = {}
+        for n in range(2, PASSES * PACK):
+            a, i = divmod(n, PACK)
+            planes[a, i] = at(n, [P, T], F32, f"plane_{a}_{i}")
+            nc.sync.dma_start(out=planes[a, i][:], in_=planes_hbm[a, i])
 
         identity = keep.tile([P, P], F32, name="identity")
         make_identity(nc, identity[:])
@@ -148,54 +148,50 @@ def tile_list_heads_hl_gelu_kernel(tc, xT, w, wgt, b, offs, out):
                     stop=(a == PASSES - 1 and part == 1),
                 )
 
-        for u in range(2):
-            moved = at(8, [P, T], F32, f"moved_{u}")
-            nc.scalar.copy(moved[:, 0:MOVE_SPLIT], pairs[u][:, T : T + MOVE_SPLIT])
-            nc.vector.tensor_copy(moved[:, MOVE_SPLIT:T], pairs[u][:, T + MOVE_SPLIT : 2 * T])
+        moved = at(8, [P, T], F32, "moved")
+        nc.scalar.copy(moved[:, 0:MOVE_SPLIT], pair[:, T : T + MOVE_SPLIT])
+        nc.vector.tensor_copy(moved[:, MOVE_SPLIT:T], pair[:, T + MOVE_SPLIT : 2 * T])
+        for u, windows in enumerate(((pair, moved), (planes[0, 2], planes[0, 3]))):
             products = at((9, 0)[u], [P, 2, S], F32, f"products_{u}")
             for j0, j1 in HALVES:
-                gather(products[:, 0, j0:j1], pairs[u], j0, j1)
+                gather(products[:, 0, j0:j1], windows[0], j0, j1)
             for j0, j1 in HALVES:
-                gather(products[:, 1, j0:j1], moved, j0, j1)
+                gather(products[:, 1, j0:j1], windows[1], j0, j1)
                 place(nc.scalar.copy, 0, 2 * u, products[:, :, j0:j1], j0, j1)
 
-        products = at(5, [P, PACK, S], F32, "products_2")
+        products = keep.tile([P, PACK, S], F32, name="products_2")
         for j0, j1 in HALVES:
-            gather(products[:, 0, j0:j1], planes[0], j0, j1)
+            gather(products[:, 0, j0:j1], planes[1, 0], j0, j1)
         quantize(0, 0, S)
         for j0, j1 in HALVES:
-            gather(products[:, 1, j0:j1], planes[1], j0, j1)
+            gather(products[:, 1, j0:j1], planes[1, 1], j0, j1)
             place(nc.scalar.copy, 1, 0, products[:, 0:2, j0 : min(j1, SPLIT)], j0, min(j1, SPLIT))
 
         reused = at(1, [P, 3 * T + 8], F32, "reused")
         bias = reused[:, 0:1]
-        for p0 in (0, P // 2):
-            nc.sync.dma_start(out=bias[p0 : p0 + P // 2], in_=b.rearrange("(p o) -> p o", o=1)[p0 : p0 + P // 2])
+        nc.sync.dma_start(out=bias, in_=b.rearrange("(p o) -> p o", o=1))
 
-        for c in (2, 0, 1, 3):
-            j0, j1 = CHUNKS[c]
-            gather(products[:, 2, j0:j1], planes[2], j0, j1)
-            if c != 2:
-                place(nc.scalar.copy, 1, 2, products[:, 2:3, j0 : min(j1, SPLIT)], j0, min(j1, SPLIT))
-        place(nc.vector.tensor_copy, 1, 2, products[:, 2:3, CHUNKS[2][0] : CHUNKS[2][1]], *CHUNKS[2])
+        for_scalar = (CHUNKS[0], CHUNKS[1], (CHUNKS[2][0], OWN[0]), (CHUNKS[3][0], SPLIT))
+        for chunk, (j0, j1) in zip(CHUNKS, for_scalar):
+            gather(products[:, 2, chunk[0] : chunk[1]], planes[1, 2], *chunk)
+            place(nc.scalar.copy, 1, 2, products[:, 2:3, j0:j1], j0, j1)
         quantize_w(0, 0, at(6, [P, M], U32, "w_codes_0_0"))
         for c in range(len(CHUNKS)):
             multiply(0, c)
 
         for c, (j0, j1) in enumerate(CHUNKS):
-            gather(products[:, 3, j0:j1] if c else first_products, planes[3], j0, j1)
+            gather(products[:, 3, j0:j1] if c else first_products, planes[1, 3], j0, j1)
         place(nc.scalar.copy, 1, 3, first_products.unsqueeze(1), *CHUNKS[0])
-        for j0, j1 in (CHUNKS[1], (CHUNKS[3][0], SPLIT)):
+        for j0, j1 in for_scalar[1:]:
             place(nc.scalar.copy, 1, 3, products[:, 3:4, j0:j1], j0, j1)
-        place(nc.vector.tensor_copy, 1, 3, products[:, 3:4, CHUNKS[2][0] : CHUNKS[2][1]], *CHUNKS[2])
+        place(nc.vector.tensor_copy, 1, 2, products[:, 2:4, OWN[0] : OWN[1]], *OWN)
         quantize(1, *CHUNKS[0])
         multiply(1, 0)
         place(nc.vector.tensor_copy, 1, 0, products[:, :, SPLIT:S], SPLIT, S)
-        for c in FINISH_ORDER[1:]:
+        for c in range(1, len(CHUNKS)):
             quantize(1, *CHUNKS[c])
             multiply(1, c)
-        for c in FINISH_ORDER:
-            j0, j1 = CHUNKS[c]
+        for c, (j0, j1) in enumerate(CHUNKS):
             result = keep.tile([M, CHUNK], F32, name=f"result_{c}", align_bytes=4 * CHUNK)
             nc.scalar.activation(result[:], acc[c][:], GELU, bias=bias)
             nc.sync.dma_start(out=out[:, j0:j1], in_=result[:])

@@ -24,8 +24,8 @@ HALF = S // 2
 HALVES = ((0, HALF), (HALF, S))
 CHUNK = 128
 CHUNKS = tuple((j0, j0 + CHUNK) for j0 in range(0, S, CHUNK))
-OWN = (3 * CHUNK - 80, 3 * CHUNK)
-SPLIT = S - 56
+OWN = (3 * CHUNK - 72, 3 * CHUNK)
+SPLIT = S - 72
 MOVE_SPLIT = 1440
 PLANE = 4 * T
 ROW_STEP = P // GROUP
@@ -114,9 +114,9 @@ def tile_list_heads_hl_gelu_kernel(tc, xT, w, wgt, b, offs, out):
         codes = [keep.tile([P, S], U32, name=f"codes_{a}", align_bytes=64) for a in range(PASSES)]
         scales = [keep.tile([P, S], U8, name=f"scales_{a}", align_bytes=64) for a in range(PASSES)]
         grouped_first = keep.tile([P, S * PACK], BF16, name="grouped_first", align_bytes=64)
-        tail_words = keep.tile([P, 2 * SPLIT + CHUNK], F32, name="tail_words", align_bytes=64)
+        tail_words = keep.tile([P, 2 * S + CHUNK], F32, name="tail_words", align_bytes=64)
         grouped = [grouped_first[:], tail_words[:, 0 : 2 * S].bitcast(BF16)]
-        first_products = tail_words[:, 2 * SPLIT : 2 * SPLIT + CHUNK]
+        first_products = tail_words[:, 2 * S - 1 : 2 * S - 1 + CHUNK]
         acc = [psum.tile([M, CHUNK], F32, name=f"acc_{c}") for c in range(len(CHUNKS))]
 
         def gather(products, window, j0, j1):
@@ -165,17 +165,18 @@ def tile_list_heads_hl_gelu_kernel(tc, xT, w, wgt, b, offs, out):
         quantize(0, 0, S)
         for j0, j1 in HALVES:
             gather(products[:, 1, j0:j1], planes[1, 1], j0, j1)
-            place(nc.scalar.copy, 1, 0, products[:, 0:2, j0 : min(j1, SPLIT)], j0, min(j1, SPLIT))
+            place(nc.scalar.copy, 1, 0, products[:, 0:2, j0:j1], j0, j1)
 
         reused = at(1, [P, 3 * T + 8], F32, "reused")
         bias = reused[:, 0:1]
         nc.sync.dma_start(out=bias, in_=b.rearrange("(p o) -> p o", o=1))
 
         for_scalar = (CHUNKS[0], CHUNKS[1], (CHUNKS[2][0], OWN[0]), (CHUNKS[3][0], SPLIT))
-        for chunk, (j0, j1) in zip(CHUNKS, for_scalar):
-            gather(products[:, 2, chunk[0] : chunk[1]], planes[1, 2], *chunk)
-            place(nc.scalar.copy, 1, 2, products[:, 2:3, j0:j1], j0, j1)
-        quantize_w(0, 0, at(6, [P, M], U32, "w_codes_0_0"))
+        early_products = at(10, [P, CHUNK], F32, "early_products")
+        for c, (j0, j1) in enumerate(for_scalar):
+            gather(products[:, 2, CHUNKS[c][0] : CHUNKS[c][1]] if c else early_products[:], planes[1, 2], *CHUNKS[c])
+            place(nc.scalar.copy, 1, 2, products[:, 2:3, j0:j1] if c else early_products[:].unsqueeze(1), j0, j1)
+        quantize_w(0, 0, at(10, [P, M], U32, "w_codes_0_0"))
         for c in range(len(CHUNKS)):
             multiply(0, c)
 
@@ -187,7 +188,7 @@ def tile_list_heads_hl_gelu_kernel(tc, xT, w, wgt, b, offs, out):
         place(nc.vector.tensor_copy, 1, 2, products[:, 2:4, OWN[0] : OWN[1]], *OWN)
         quantize(1, *CHUNKS[0])
         multiply(1, 0)
-        place(nc.vector.tensor_copy, 1, 0, products[:, :, SPLIT:S], SPLIT, S)
+        place(nc.vector.tensor_copy, 1, 2, products[:, 2:4, SPLIT:S], SPLIT, S)
         for c in range(1, len(CHUNKS)):
             quantize(1, *CHUNKS[c])
             multiply(1, c)

@@ -111,7 +111,7 @@ def tile_list_heads_hl_gelu_kernel(tc, xT, w, wgt, b, offs, out):
         for a, part in ((0, 1), (1, 0), (1, 1)):
             quantize_w(a, part, keep.tile([P, M], U32, name=f"w_codes_{a}_{part}", align_bytes=64))
 
-        codes = [keep.tile([P, S], U32, name=f"codes_{a}", align_bytes=64) for a in range(PASSES)]
+        codes = [placed.tile([P, S], U32, name="codes_0", align_bytes=64, offset=9 * PLANE // 2), keep.tile([P, S], U32, name="codes_1", align_bytes=64)]
         scales = [keep.tile([P, S], U8, name=f"scales_{a}", align_bytes=64) for a in range(PASSES)]
         grouped_first = keep.tile([P, S * PACK], BF16, name="grouped_first", align_bytes=64)
         tail_words = keep.tile([P, 2 * S + CHUNK], F32, name="tail_words", align_bytes=64)

@@ -21,6 +21,7 @@ PACK = 4
 PASSES = K // (P * PACK)
 GROUP = 16
 HALF = S // 2
+WHOLE = ((0, S),)
 HALVES = ((0, HALF), (HALF, S))
 CHUNK = 128
 CHUNKS = tuple((j0, j0 + CHUNK) for j0 in range(0, S, CHUNK))
@@ -45,7 +46,7 @@ def tile_list_heads_hl_gelu_kernel(tc, xT, w, wgt, b, offs, out):
         def at(planes_in, shape, dtype, name):
             return placed.tile(shape, dtype, name=name, align_bytes=PLANE, offset=planes_in * PLANE)
 
-        rows = keep.tile([P, HALF], F32, name="rows", align_bytes=4 * HALF)
+        rows = at(11, [P, HALF], F32, "rows")
         nc.vector.memset(rows[:], 0.0)
         w_raw = keep.tile([P, PASSES, PACK, M], F32, name="w_raw", align_bytes=4 * PASSES * PACK * M)
         nc.sync.dma_start(out=w_raw[:], in_=w.rearrange("(a p i) n -> p a i n", p=P, i=PACK))
@@ -64,52 +65,43 @@ def tile_list_heads_hl_gelu_kernel(tc, xT, w, wgt, b, offs, out):
 
         identity = keep.tile([P, P], F32, name="identity")
         make_identity(nc, identity[:])
-        zero = keep.tile([P, 1], F32, name="zero")
-        nc.vector.memset(zero[:], 0.0)
         warm = keep.tile([P, 1], F32, name="warm")
-        nc.scalar.activation(warm[:], zero[:], GELU)
+        nc.scalar.activation(warm[:], identity[:, 0:1], GELU)
 
         blocks = HALF // P
         columns_ps = psum.tile([P, blocks, P], F32, name="columns_ps")
         for c in range(blocks):
             nc.tensor.transpose(columns_ps[:, c, :], rows[:, c * P : (c + 1) * P], identity[:])
         weights = keep.tile([P, S], F32, name="weights")
-        repeated = at(8, [P, 2, blocks, P // GROUP, GROUP], F32, "repeated")
+        repeated = keep.tile([P, 2, blocks, P // GROUP, GROUP], F32, name="repeated")
+        nc.vector.tensor_copy(
+            repeated[:],
+            columns_ps[:, :, 0:P:ROW_STEP]
+            .rearrange("p c (g h) -> p h c g", h=2)
+            .unsqueeze(4)
+            .to_broadcast([P, 2, blocks, P // GROUP, GROUP]),
+        )
+        weights_ps = psum.tile([P, S], F32, name="weights_ps")
         for h in range(2):
-            nc.scalar.copy(
-                repeated[:, h],
-                columns_ps[:, :, ROW_STEP * h : P : 2 * ROW_STEP]
-                .unsqueeze(3)
-                .to_broadcast([P, blocks, P // GROUP, GROUP]),
-            )
-        for h in range(2):
-            weights_ps = psum.tile([P, HALF], F32, name=f"weights_ps_{h}")
             for c in range(blocks):
-                nc.tensor.transpose(
-                    weights_ps[:, c * P : (c + 1) * P], repeated[:, h, c].rearrange("p g r -> p (g r)"), identity[:]
-                )
-            nc.scalar.copy(weights[:, h * HALF : (h + 1) * HALF], weights_ps[:])
+                j0 = h * HALF + c * P
+                nc.tensor.transpose(weights_ps[:, j0 : j0 + P], repeated[:, h, c].rearrange("p g r -> p (g r)"), identity[:])
+        nc.vector.tensor_copy(weights[:], weights_ps[:])
 
         hi_bits = keep.tile([P, PASSES, PACK, M], I32, name="hi_bits")
         nc.vector.tensor_scalar(hi_bits[:], w_raw[:].bitcast(I32), HEAD_BITS, None, AND)
-        w_grouped = keep.tile([P, PASSES, 2, M, PACK], BF16, name="w_grouped", align_bytes=64)
-        for a in range(PASSES):
-            hi_view = hi_bits[:, a].bitcast(F32).rearrange("p i n -> p n i")
-            nc.vector.tensor_tensor(w_grouped[:, a, 0], w_raw[:, a].rearrange("p i n -> p n i"), hi_view, SUB)
-            nc.vector.tensor_copy(w_grouped[:, a, 1], hi_view)
+        w_grouped = at(11, [P, PASSES, 2, M, PACK], BF16, "w_grouped")
+        hi_view = hi_bits[:].bitcast(F32).rearrange("p a i n -> p a n i")
+        nc.vector.tensor_tensor(w_grouped[:, :, 0], w_raw[:].rearrange("p a i n -> p a n i"), hi_view, SUB)
+        nc.vector.tensor_copy(w_grouped[:, :, 1], hi_view)
+        w_flat = w_grouped[:].rearrange("p a r n i -> p (a r n i)")
+        early_codes = keep.tile([P, 3 * M], U32, name="early_codes", align_bytes=64)
+        early_scales = keep.tile([P, 3 * M], U8, name="early_scales", align_bytes=64)
+        nc.vector.quantize_mx(out=early_codes[:].bitcast(FP8X4), scales=early_scales[:], in_=w_flat[:, M * PACK :])
         w_codes, w_scales = {}, {}
-
-        def quantize_w(a, part, words):
-            w_codes[a, part] = words
-            w_scales[a, part] = keep.tile([P, M], U8, name=f"w_scales_{a}_{part}", align_bytes=64)
-            nc.vector.quantize_mx(
-                out=words[:].bitcast(FP8X4),
-                scales=w_scales[a, part][:],
-                in_=w_grouped[:, a, part].rearrange("p n i -> p (n i)"),
-            )
-
-        for a, part in ((0, 1), (1, 0), (1, 1)):
-            quantize_w(a, part, keep.tile([P, M], U32, name=f"w_codes_{a}_{part}", align_bytes=64))
+        for n, operand in enumerate(((0, 1), (1, 0), (1, 1))):
+            w_codes[operand] = early_codes[:, n * M : (n + 1) * M]
+            w_scales[operand] = early_scales[:, n * M : (n + 1) * M]
 
         codes = [placed.tile([P, S], U32, name="codes_0", align_bytes=64, offset=9 * PLANE // 2), keep.tile([P, S], U32, name="codes_1", align_bytes=64)]
         scales = [keep.tile([P, S], U8, name=f"scales_{a}", align_bytes=64) for a in range(PASSES)]
@@ -140,8 +132,8 @@ def tile_list_heads_hl_gelu_kernel(tc, xT, w, wgt, b, offs, out):
             for part in range(2):
                 nc.tensor.matmul_mx(
                     out=acc[c][:],
-                    lhsT=w_codes[a, part][:].bitcast(FP8X4),
-                    lhsT_scale=w_scales[a, part][:],
+                    lhsT=w_codes[a, part].bitcast(FP8X4),
+                    lhsT_scale=w_scales[a, part],
                     rhs=codes[a][:, j0:j1].bitcast(FP8X4),
                     rhs_scale=scales[a][:, j0:j1],
                     start=(a == 0 and part == 0),
@@ -153,15 +145,13 @@ def tile_list_heads_hl_gelu_kernel(tc, xT, w, wgt, b, offs, out):
         nc.vector.tensor_copy(moved[:, MOVE_SPLIT:T], pair[:, T + MOVE_SPLIT : 2 * T])
         for u, windows in enumerate(((pair, moved), (planes[0, 2], planes[0, 3]))):
             products = at((9, 0)[u], [P, 2, S], F32, f"products_{u}")
-            for j0, j1 in HALVES:
+            for j0, j1 in (HALVES, WHOLE)[u]:
                 gather(products[:, 0, j0:j1], windows[0], j0, j1)
-            for j0, j1 in HALVES:
-                gather(products[:, 1, j0:j1], windows[1], j0, j1)
-                place(nc.scalar.copy, 0, 2 * u, products[:, :, j0:j1], j0, j1)
+            gather(products[:, 1], windows[1], 0, S)
+            place(nc.scalar.copy, 0, 2 * u, products[:], 0, S)
 
         products = keep.tile([P, PACK, S], F32, name="products_2")
-        for j0, j1 in HALVES:
-            gather(products[:, 0, j0:j1], planes[1, 0], j0, j1)
+        gather(products[:, 0], planes[1, 0], 0, S)
         quantize(0, 0, S)
         for j0, j1 in HALVES:
             gather(products[:, 1, j0:j1], planes[1, 1], j0, j1)
@@ -173,10 +163,21 @@ def tile_list_heads_hl_gelu_kernel(tc, xT, w, wgt, b, offs, out):
 
         for_scalar = (CHUNKS[0], CHUNKS[1], (CHUNKS[2][0], OWN[0]), (CHUNKS[3][0], SPLIT))
         early_products = at(10, [P, CHUNK], F32, "early_products")
-        for c, (j0, j1) in enumerate(for_scalar):
-            gather(products[:, 2, CHUNKS[c][0] : CHUNKS[c][1]] if c else early_products[:], planes[1, 2], *CHUNKS[c])
-            place(nc.scalar.copy, 1, 2, products[:, 2:3, j0:j1] if c else early_products[:].unsqueeze(1), j0, j1)
-        quantize_w(0, 0, at(10, [P, M], U32, "w_codes_0_0"))
+        for c, (j0, j1) in enumerate(CHUNKS[0:2]):
+            piece = products[:, 2, j0:j1] if c else early_products[:]
+            gather(piece, planes[1, 2], j0, j1)
+            place(nc.scalar.copy, 1, 2, piece.unsqueeze(1), j0, j1)
+        gather(products[:, 2, HALF:S], planes[1, 2], HALF, S)
+        heads = SPLIT - CHUNKS[3][0]
+        nc.scalar.copy(
+            grouped[1][:, HALF * PACK :].rearrange("p (c j i) -> p c j i", c=2, i=PACK)[:, :, 0:heads, 2],
+            products[:, 2, HALF:].rearrange("p (c j) -> p c j", c=2)[:, :, 0:heads],
+        )
+        late_codes = at(10, [P, M], U32, "late_codes")
+        late_scales = keep.tile([P, M], U8, name="late_scales", align_bytes=64)
+        nc.vector.quantize_mx(out=late_codes[:].bitcast(FP8X4), scales=late_scales[:], in_=w_flat[:, 0 : M * PACK])
+        w_codes[0, 0] = late_codes[:]
+        w_scales[0, 0] = late_scales[:]
         for c in range(len(CHUNKS)):
             multiply(0, c)
 

@@ -180,6 +180,17 @@ def tile_list_heads_hl_gelu_kernel(tc, xT, w, wgt, b, offs, out):
         w_scales[0, 0] = late_scales[:]
         for c in range(len(CHUNKS)):
             multiply(0, c)
+        warm_ps = psum.tile([M, 2, CHUNK], F32, name="warm_ps")
+        for r, width in enumerate((CHUNK, CHUNK // 2)):
+            nc.tensor.matmul_mx(
+                out=warm_ps[:, r, 0:width],
+                lhsT=w_codes[0, 0].bitcast(FP8X4),
+                lhsT_scale=w_scales[0, 0],
+                rhs=codes[0][:, 0:width].bitcast(FP8X4),
+                rhs_scale=scales[0][:, 0:width],
+                start=True,
+                stop=True,
+            )
 
         for c, (j0, j1) in enumerate(CHUNKS):
             gather(products[:, 3, j0:j1] if c else first_products, planes[1, 3], j0, j1)

@@ -25,8 +25,9 @@ WHOLE = ((0, S),)
 HALVES = ((0, HALF), (HALF, S))
 CHUNK = 128
 CHUNKS = tuple((j0, j0 + CHUNK) for j0 in range(0, S, CHUNK))
-OWN = (3 * CHUNK - 72, 3 * CHUNK)
-SPLIT = S - 72
+EDGE = CHUNK // 2
+EIGHTHS = tuple((j0, j0 + EDGE) for j0 in range(HALF, S, EDGE))
+FOR_SCALAR = (CHUNKS[0], CHUNKS[1], EIGHTHS[0], EIGHTHS[3])
 MOVE_SPLIT = 1440
 PLANE = 4 * T
 ROW_STEP = P // GROUP
@@ -106,9 +107,16 @@ def tile_list_heads_hl_gelu_kernel(tc, xT, w, wgt, b, offs, out):
         codes = [placed.tile([P, S], U32, name="codes_0", align_bytes=64, offset=9 * PLANE // 2), keep.tile([P, S], U32, name="codes_1", align_bytes=64)]
         scales = [keep.tile([P, S], U8, name=f"scales_{a}", align_bytes=64) for a in range(PASSES)]
         grouped_first = keep.tile([P, S * PACK], BF16, name="grouped_first", align_bytes=64)
-        tail_words = keep.tile([P, 2 * S + CHUNK], F32, name="tail_words", align_bytes=64)
-        grouped = [grouped_first[:], tail_words[:, 0 : 2 * S].bitcast(BF16)]
-        first_products = tail_words[:, 2 * S - 1 : 2 * S - 1 + CHUNK]
+        grouped_low = keep.tile([P, HALF * PACK], BF16, name="grouped_low", align_bytes=64)
+        tail_words = keep.tile([P, len(EIGHTHS) * 2 * CHUNK], F32, name="tail_words", align_bytes=64)
+        grouped_high = tail_words[:].bitcast(BF16).rearrange("p (r u j i) -> p r u j i", u=2, j=EDGE, i=PACK)[:, :, 0]
+        held_products = [tail_words[:, (2 * r + 1) * CHUNK - 1 : (2 * r + 2) * CHUNK - 1] for r in (1, 2)]
+
+        def rounded(a, j0, j1):
+            if a == 0 or j1 <= HALF:
+                return (grouped_first, grouped_low)[a][:, j0 * PACK : j1 * PACK]
+            return grouped_high[:, (j0 - HALF) // EDGE].rearrange("p j i -> p (j i)")
+
         acc = [psum.tile([M, CHUNK], F32, name=f"acc_{c}") for c in range(len(CHUNKS))]
 
         def gather(products, window, j0, j1):
@@ -117,14 +125,14 @@ def tile_list_heads_hl_gelu_kernel(tc, xT, w, wgt, b, offs, out):
             )
 
         def place(copy, a, i0, products, j0, j1):
-            slots = grouped[a].rearrange("p (j i) -> p j i", i=PACK)
-            copy(slots[:, j0:j1, i0 : i0 + products.shape[1]], products.rearrange("p i j -> p j i"))
+            slots = rounded(a, j0, j1).rearrange("p (j i) -> p j i", i=PACK)
+            copy(slots[:, :, i0 : i0 + products.shape[1]], products.rearrange("p i j -> p j i"))
 
         def quantize(a, j0, j1):
             nc.vector.quantize_mx(
                 out=codes[a][:, j0:j1].bitcast(FP8X4),
                 scales=scales[a][:, j0:j1],
-                in_=grouped[a][:, j0 * PACK : j1 * PACK],
+                in_=rounded(a, j0, j1),
             )
 
         def multiply(a, c):
@@ -155,24 +163,20 @@ def tile_list_heads_hl_gelu_kernel(tc, xT, w, wgt, b, offs, out):
         quantize(0, 0, S)
         for j0, j1 in HALVES:
             gather(products[:, 1, j0:j1], planes[1, 1], j0, j1)
-            place(nc.scalar.copy, 1, 0, products[:, 0:2, j0:j1], j0, j1)
+        place(nc.scalar.copy, 1, 0, products[:, 0:2, 0:HALF], 0, HALF)
+        nc.scalar.copy(grouped_high[:, :, :, 0:2], products[:, 0:2, HALF:S].rearrange("p i (r j) -> p r j i", j=EDGE))
 
         reused = at(1, [P, 3 * T + 8], F32, "reused")
         bias = reused[:, 0:1]
         nc.sync.dma_start(out=bias, in_=b.rearrange("(p o) -> p o", o=1))
 
-        for_scalar = (CHUNKS[0], CHUNKS[1], (CHUNKS[2][0], OWN[0]), (CHUNKS[3][0], SPLIT))
         early_products = at(10, [P, CHUNK], F32, "early_products")
         for c, (j0, j1) in enumerate(CHUNKS[0:2]):
             piece = products[:, 2, j0:j1] if c else early_products[:]
             gather(piece, planes[1, 2], j0, j1)
             place(nc.scalar.copy, 1, 2, piece.unsqueeze(1), j0, j1)
         gather(products[:, 2, HALF:S], planes[1, 2], HALF, S)
-        heads = SPLIT - CHUNKS[3][0]
-        nc.scalar.copy(
-            grouped[1][:, HALF * PACK :].rearrange("p (c j i) -> p c j i", c=2, i=PACK)[:, :, 0:heads, 2],
-            products[:, 2, HALF:].rearrange("p (c j) -> p c j", c=2)[:, :, 0:heads],
-        )
+        nc.scalar.copy(grouped_high[:, 0:4:3, :, 2], products[:, 2, HALF:S].rearrange("p (r j) -> p r j", j=EDGE)[:, 0:4:3])
         late_codes = at(10, [P, M], U32, "late_codes")
         late_scales = keep.tile([P, M], U8, name="late_scales", align_bytes=64)
         nc.vector.quantize_mx(out=late_codes[:].bitcast(FP8X4), scales=late_scales[:], in_=w_flat[:, 0 : M * PACK])
@@ -193,17 +197,20 @@ def tile_list_heads_hl_gelu_kernel(tc, xT, w, wgt, b, offs, out):
             )
 
         for c, (j0, j1) in enumerate(CHUNKS):
-            gather(products[:, 3, j0:j1] if c else first_products, planes[1, 3], j0, j1)
-        place(nc.scalar.copy, 1, 3, first_products.unsqueeze(1), *CHUNKS[0])
-        for j0, j1 in for_scalar[1:]:
-            place(nc.scalar.copy, 1, 3, products[:, 3:4, j0:j1], j0, j1)
-        place(nc.vector.tensor_copy, 1, 2, products[:, 2:4, OWN[0] : OWN[1]], *OWN)
-        quantize(1, *CHUNKS[0])
-        multiply(1, 0)
-        place(nc.vector.tensor_copy, 1, 2, products[:, 2:4, SPLIT:S], SPLIT, S)
-        for c in range(1, len(CHUNKS)):
+            gather(held_products[c] if c < 2 else products[:, 3, j0:j1], planes[1, 3], j0, j1)
+        for c, (j0, j1) in enumerate(FOR_SCALAR):
+            place(nc.scalar.copy, 1, 3, held_products[c].unsqueeze(1) if c < 2 else products[:, 3:4, j0:j1], j0, j1)
+        for c in range(2):
             quantize(1, *CHUNKS[c])
             multiply(1, c)
+            j0, j1 = EIGHTHS[1 + c]
+            place(nc.vector.tensor_copy, 1, 2, products[:, 2:4, j0:j1], j0, j1)
+        for r in (0, 1):
+            quantize(1, *EIGHTHS[r])
+        multiply(1, 2)
+        for r in (3, 2):
+            quantize(1, *EIGHTHS[r])
+        multiply(1, 3)
         for c, (j0, j1) in enumerate(CHUNKS):
             result = keep.tile([M, CHUNK], F32, name=f"result_{c}", align_bytes=4 * CHUNK)
             nc.scalar.activation(result[:], acc[c][:], GELU, bias=bias)

from contextlib import ExitStack

import concourse.mybir as mybir
from concourse.masks import make_identity

F32 = mybir.dt.float32
BF16 = mybir.dt.bfloat16
I32 = mybir.dt.int32
U32 = mybir.dt.uint32
U16 = mybir.dt.uint16
U8 = mybir.dt.uint8
FP8X4 = mybir.dt.float8_e4m3fn_x4
MULT = mybir.AluOpType.mult
SUB = mybir.AluOpType.subtract
AND = mybir.AluOpType.bitwise_and
GELU = mybir.ActivationFunctionType.Gelu_apprx_tanh

K, M, T, S = 1024, 128, 2048, 512
P = 128
PACK = 4
PASSES = K // (P * PACK)
GROUP = 16
HALF = S // 2
WHOLE = ((0, S),)
HALVES = ((0, HALF), (HALF, S))
CHUNK = 128
CHUNKS = tuple((j0, j0 + CHUNK) for j0 in range(0, S, CHUNK))
EDGE = CHUNK // 2
EIGHTHS = tuple((j0, j0 + EDGE) for j0 in range(HALF, S, EDGE))
FOR_SCALAR = (CHUNKS[0], CHUNKS[1], EIGHTHS[0], EIGHTHS[3])
MOVE_SPLIT = 1440
PLANE = 4 * T
ROW_STEP = P // GROUP
HEAD_BITS = -(1 << 20)

FLOPS = 2 * 2 * K * M * S
BYTES = 4 * (K * T + K * M + P // GROUP * S + M + M * S) + 2 * P * (S // GROUP)


def tile_list_heads_hl_gelu_kernel(tc, xT, w, wgt, b, offs, out):
    nc = tc.nc
    with ExitStack() as ctx:
        keep = ctx.enter_context(tc.tile_pool(name="keep", bufs=1))
        placed = ctx.enter_context(tc.tile_pool(name="placed", bufs=1))
        psum = ctx.enter_context(tc.psum_pool(name="psum", bufs=1))

        def at(planes_in, shape, dtype, name):
            return placed.tile(shape, dtype, name=name, align_bytes=PLANE, offset=planes_in * PLANE)

        rows = at(11, [P, HALF], F32, "rows")
        nc.vector.memset(rows[:], 0.0)
        w_raw = keep.tile([P, PASSES, PACK, M], F32, name="w_raw", align_bytes=4 * PASSES * PACK * M)
        nc.sync.dma_start(out=w_raw[:], in_=w.rearrange("(a p i) n -> p a i n", p=P, i=PACK))
        offsets = keep.tile([P, S // GROUP], U16, name="offsets", align_bytes=2 * S // GROUP)
        nc.sync.dma_start(offsets[:], offs)
        half_rows = wgt.rearrange("p (h j) -> (p h) j", h=2)
        nc.sync.dma_start(out=rows[0:P:ROW_STEP, :], in_=half_rows[0 : 2 * P : GROUP + 1, :])
        planes_hbm = xT.rearrange("(a p i) t -> a i p t", p=P, i=PACK)
        pair = at(0, [P, 2 * T], F32, "pair")
        nc.sync.dma_start(out=pair[:], in_=xT.rearrange("(a p u e) t -> a u p (e t)", p=P, u=2, e=2)[0, 0])
        planes = {}
        for n in range(2, PASSES * PACK):
            a, i = divmod(n, PACK)
            planes[a, i] = at(n, [P, T], F32, f"plane_{a}_{i}")
            nc.sync.dma_start(out=planes[a, i][:], in_=planes_hbm[a, i])

        identity = keep.tile([P, P], F32, name="identity")
        make_identity(nc, identity[:])
        warm = keep.tile([P, 1], F32, name="warm")
        nc.scalar.activation(warm[:], identity[:, 0:1], GELU)

        blocks = HALF // P
        columns_ps = psum.tile([P, blocks, P], F32, name="columns_ps")
        for c in range(blocks):
            nc.tensor.transpose(columns_ps[:, c, :], rows[:, c * P : (c + 1) * P], identity[:])
        weights = keep.tile([P, S], F32, name="weights")
        repeated = keep.tile([P, 2, blocks, P // GROUP, GROUP], F32, name="repeated")
        nc.vector.tensor_copy(
            repeated[:],
            columns_ps[:, :, 0:P:ROW_STEP]
            .rearrange("p c (g h) -> p h c g", h=2)
            .unsqueeze(4)
            .to_broadcast([P, 2, blocks, P // GROUP, GROUP]),
        )
        weights_ps = psum.tile([P, S], F32, name="weights_ps")
        for h in range(2):
            for c in range(blocks):
                j0 = h * HALF + c * P
                nc.tensor.transpose(weights_ps[:, j0 : j0 + P], repeated[:, h, c].rearrange("p g r -> p (g r)"), identity[:])
        nc.vector.tensor_copy(weights[:], weights_ps[:])

        hi_bits = keep.tile([P, PASSES, PACK, M], I32, name="hi_bits")
        nc.vector.tensor_scalar(hi_bits[:], w_raw[:].bitcast(I32), HEAD_BITS, None, AND)
        w_grouped = at(11, [P, PASSES, 2, M, PACK], BF16, "w_grouped")
        hi_view = hi_bits[:].bitcast(F32).rearrange("p a i n -> p a n i")
        nc.vector.tensor_tensor(w_grouped[:, :, 0], w_raw[:].rearrange("p a i n -> p a n i"), hi_view, SUB)
        nc.vector.tensor_copy(w_grouped[:, :, 1], hi_view)
        w_flat = w_grouped[:].rearrange("p a r n i -> p (a r n i)")
        early_codes = keep.tile([P, 3 * M], U32, name="early_codes", align_bytes=64)
        early_scales = keep.tile([P, 3 * M], U8, name="early_scales", align_bytes=64)
        nc.vector.quantize_mx(out=early_codes[:].bitcast(FP8X4), scales=early_scales[:], in_=w_flat[:, M * PACK :])
        w_codes, w_scales = {}, {}
        for n, operand in enumerate(((0, 1), (1, 0), (1, 1))):
            w_codes[operand] = early_codes[:, n * M : (n + 1) * M]
            w_scales[operand] = early_scales[:, n * M : (n + 1) * M]

        codes = [placed.tile([P, S], U32, name="codes_0", align_bytes=64, offset=9 * PLANE // 2), keep.tile([P, S], U32, name="codes_1", align_bytes=64)]
        scales = [keep.tile([P, S], U8, name=f"scales_{a}", align_bytes=64) for a in range(PASSES)]
        grouped_first = keep.tile([P, S * PACK], BF16, name="grouped_first", align_bytes=64)
        grouped_low = keep.tile([P, HALF * PACK], BF16, name="grouped_low", align_bytes=64)
        tail_words = keep.tile([P, len(EIGHTHS) * 2 * CHUNK], F32, name="tail_words", align_bytes=64)
        grouped_high = tail_words[:].bitcast(BF16).rearrange("p (r u j i) -> p r u j i", u=2, j=EDGE, i=PACK)[:, :, 0]
        held_products = [tail_words[:, (2 * r + 1) * CHUNK - 1 : (2 * r + 2) * CHUNK - 1] for r in (1, 2)]

        def rounded(a, j0, j1):
            if a == 0 or j1 <= HALF:
                return (grouped_first, grouped_low)[a][:, j0 * PACK : j1 * PACK]
            return grouped_high[:, (j0 - HALF) // EDGE].rearrange("p j i -> p (j i)")

        acc = [psum.tile([M, CHUNK], F32, name=f"acc_{c}") for c in range(len(CHUNKS))]

        def gather(products, window, j0, j1):
            nc.vector.tensor_tensor(
                products, window[:].indirect(offsets[:, j0 // GROUP : j1 // GROUP]), weights[:, j0:j1], MULT
            )

        def place(copy, a, i0, products, j0, j1):
            slots = rounded(a, j0, j1).rearrange("p (j i) -> p j i", i=PACK)
            copy(slots[:, :, i0 : i0 + products.shape[1]], products.rearrange("p i j -> p j i"))

        def quantize(a, j0, j1):
            nc.vector.quantize_mx(
                out=codes[a][:, j0:j1].bitcast(FP8X4),
                scales=scales[a][:, j0:j1],
                in_=rounded(a, j0, j1),
            )

        def multiply(a, c):
            j0, j1 = CHUNKS[c]
            for part in range(2):
                nc.tensor.matmul_mx(
                    out=acc[c][:],
                    lhsT=w_codes[a, part].bitcast(FP8X4),
                    lhsT_scale=w_scales[a, part],
                    rhs=codes[a][:, j0:j1].bitcast(FP8X4),
                    rhs_scale=scales[a][:, j0:j1],
                    start=(a == 0 and part == 0),
                    stop=(a == PASSES - 1 and part == 1),
                )

        moved = at(8, [P, T], F32, "moved")
        nc.scalar.copy(moved[:, 0:MOVE_SPLIT], pair[:, T : T + MOVE_SPLIT])
        nc.vector.tensor_copy(moved[:, MOVE_SPLIT:T], pair[:, T + MOVE_SPLIT : 2 * T])
        for u, windows in enumerate(((pair, moved), (planes[0, 2], planes[0, 3]))):
            products = at((9, 0)[u], [P, 2, S], F32, f"products_{u}")
            for j0, j1 in (HALVES, WHOLE)[u]:
                gather(products[:, 0, j0:j1], windows[0], j0, j1)
            gather(products[:, 1], windows[1], 0, S)
            place(nc.scalar.copy, 0, 2 * u, products[:], 0, S)

        products = keep.tile([P, PACK, S], F32, name="products_2")
        gather(products[:, 0], planes[1, 0], 0, S)
        quantize(0, 0, S)
        for j0, j1 in HALVES:
            gather(products[:, 1, j0:j1], planes[1, 1], j0, j1)
        place(nc.scalar.copy, 1, 0, products[:, 0:2, 0:HALF], 0, HALF)
        nc.scalar.copy(grouped_high[:, :, :, 0:2], products[:, 0:2, HALF:S].rearrange("p i (r j) -> p r j i", j=EDGE))

        reused = at(1, [P, 3 * T + 8], F32, "reused")
        bias = reused[:, 0:1]
        nc.sync.dma_start(out=bias, in_=b.rearrange("(p o) -> p o", o=1))

        early_products = at(10, [P, CHUNK], F32, "early_products")
        for c, (j0, j1) in enumerate(CHUNKS[0:2]):
            piece = products[:, 2, j0:j1] if c else early_products[:]
            gather(piece, planes[1, 2], j0, j1)
            place(nc.scalar.copy, 1, 2, piece.unsqueeze(1), j0, j1)
        gather(products[:, 2, HALF:S], planes[1, 2], HALF, S)
        nc.scalar.copy(grouped_high[:, 0:4:3, :, 2], products[:, 2, HALF:S].rearrange("p (r j) -> p r j", j=EDGE)[:, 0:4:3])
        late_codes = at(10, [P, M], U32, "late_codes")
        late_scales = keep.tile([P, M], U8, name="late_scales", align_bytes=64)
        nc.vector.quantize_mx(out=late_codes[:].bitcast(FP8X4), scales=late_scales[:], in_=w_flat[:, 0 : M * PACK])
        w_codes[0, 0] = late_codes[:]
        w_scales[0, 0] = late_scales[:]
        for c in range(len(CHUNKS)):
            multiply(0, c)
        warm_ps = psum.tile([M, 2, CHUNK], F32, name="warm_ps")
        for r, width in enumerate((CHUNK, CHUNK // 2)):
            nc.tensor.matmul_mx(
                out=warm_ps[:, r, 0:width],
                lhsT=w_codes[0, 0].bitcast(FP8X4),
                lhsT_scale=w_scales[0, 0],
                rhs=codes[0][:, 0:width].bitcast(FP8X4),
                rhs_scale=scales[0][:, 0:width],
                start=True,
                stop=True,
            )

        for c, (j0, j1) in enumerate(CHUNKS):
            gather(held_products[c] if c < 2 else products[:, 3, j0:j1], planes[1, 3], j0, j1)
        for c, (j0, j1) in enumerate(FOR_SCALAR):
            place(nc.scalar.copy, 1, 3, held_products[c].unsqueeze(1) if c < 2 else products[:, 3:4, j0:j1], j0, j1)
        for c in range(2):
            quantize(1, *CHUNKS[c])
            multiply(1, c)
            j0, j1 = EIGHTHS[1 + c]
            place(nc.vector.tensor_copy, 1, 2, products[:, 2:4, j0:j1], j0, j1)
        for r in (0, 1):
            quantize(1, *EIGHTHS[r])
        multiply(1, 2)
        for r in (3, 2):
            quantize(1, *EIGHTHS[r])
        multiply(1, 3)
        for c, (j0, j1) in enumerate(CHUNKS):
            result = keep.tile([M, CHUNK], F32, name=f"result_{c}", align_bytes=4 * CHUNK)
            nc.scalar.activation(result[:], acc[c][:], GELU, bias=bias)
            nc.sync.dma_start(out=out[:, j0:j1], in_=result[:])
